import numpy as np
import ml_dtypes


def mxq(x, axis, fmt="e4m3"):
    dtype, down = {"e4m3": (ml_dtypes.float8_e4m3fn, 7), "e5m2": (ml_dtypes.float8_e5m2, 14)}[fmt]
    v = np.moveaxis(np.asarray(x, np.float32).astype(ml_dtypes.bfloat16).astype(np.float64), axis, -1)
    blocks = v.reshape(v.shape[:-1] + (-1, 32))
    amax = np.abs(blocks).max(-1, keepdims=True)
    byte = np.maximum(np.where(amax > 0, np.frexp(amax)[1] - 1 + 127, 0) - down, 1)
    scale = np.exp2(byte - 127.0)
    codes = (blocks / scale).astype(np.float32).astype(dtype).astype(np.float64)
    return np.moveaxis((codes * scale).reshape(v.shape), -1, axis)


WIDE = False


def mx_kscale(k):
    if not WIDE:
        return np.ones(k)
    levels = np.array([10, -10, 5, -5, 0])
    if k % 512:
        return np.exp2(np.random.permutation(np.resize(levels, k // 32))).repeat(32)
    a = np.empty((k // 512, 16))
    for p in range(k // 512):
        a[p, :8] = np.random.permutation(np.resize(levels, 8))
        for g in range(8):
            far = levels[np.abs(levels - a[p, g]) >= 10]
            a[p, g + 8] = far[np.random.randint(len(far))]
    return np.exp2(a.ravel()).repeat(32)


def f64(x):
    return np.asarray(x).astype(np.float64)


def striped(idx):
    return np.tile(idx.reshape(-1, 16).T, (8, 1)).astype(np.uint16)


def unstriped(offs):
    return offs[:16].T.reshape(-1).astype(np.int64)


E2M1 = np.array([0.0, 0.5, 1.0, 1.5, 2.0, 3.0, 4.0, 6.0, -0.0, -0.5, -1.0, -1.5, -2.0, -3.0, -4.0, -6.0])


def pack_weight(w, fmt):
    k, n = w.shape
    w = f64(np.asarray(w, np.float32).astype(ml_dtypes.bfloat16)).reshape(k // 32, 32, n)
    amax = np.abs(w).max(1)
    if fmt == "e4m3":
        byte = np.frexp(amax)[1] - 1 + 127 - 7
    else:
        mant, ex = np.frexp(amax / 6.0)
        byte = np.where(mant > 0.5, ex, ex - 1) + 127
    byte = np.clip(np.where(amax > 0, byte, 1), 1, 254)
    scaled = (w * np.exp2(127.0 - byte)[:, None, :]).reshape(k, n).astype(np.float32)
    by_word = np.ascontiguousarray(scaled.reshape(k // 512, 128, 4, n).transpose(0, 1, 3, 2))
    if fmt == "e4m3":
        words = by_word.astype(ml_dtypes.float8_e4m3fn).view(np.uint8)
    else:
        c = by_word.astype(ml_dtypes.float4_e2m1fn).view(np.uint8) & 0xF
        words = (c[..., 0::2] | (c[..., 1::2] << 4)).reshape(k // 512, 128, 2 * n)
    return np.ascontiguousarray(words), np.ascontiguousarray(byte.astype(np.uint8).reshape(k // 512, 16, n))


def unpack_weight(words, scales, fmt):
    g, _, n = scales.shape
    words = np.ascontiguousarray(words).reshape(g, 128, n, -1)
    if fmt == "e4m3":
        vals = words.view(ml_dtypes.float8_e4m3fn).astype(np.float64)
    else:
        nib = np.empty((g, 128, n, 4), np.uint8)
        nib[..., 0::2] = words & 0xF
        nib[..., 1::2] = words >> 4
        vals = E2M1[nib]
    vals = vals * np.repeat(np.exp2(scales.astype(np.float64) - 127.0), 8, axis=1)[..., None]
    return vals.transpose(0, 1, 3, 2).reshape(g * 512, n)


def relu2(v):
    return np.maximum(v, 0.0) ** 2


K, T, E, C, N = 1024, 1024, 8, 256, 512
R = 8


def by_expert(wq, xq):
    return np.concatenate([wq[e].T @ xq[:, e * C:(e + 1) * C] for e in range(E)], axis=1)


def setup_inputs():
    n = np.random.standard_normal
    s = mx_kscale(K)[:, None]
    slot_token = np.concatenate([r * (T // R) + np.random.permutation(T // R)[:C // R] for e in range(E) for r in range(R)])
    w = [pack_weight(m, "e2m1") for m in n((E, K, N)) / np.sqrt(K) / s[None]]
    return {
        "xT": (n((K, T)) * s).astype(np.float32),
        "w_words": np.stack([m[0] for m in w]),
        "w_scales": np.stack([m[1] for m in w]),
        "b": (0.3 * n((N, E))).astype(np.float32),
        "offs": striped(slot_token),
    }


def reference(xT, w_words, w_scales, b, offs):
    idx = unstriped(offs)
    w = np.stack([unpack_weight(w_words[e], w_scales[e], "e2m1") for e in range(E)])
    xq = mxq(f64(xT)[:, idx], 0, "e4m3")
    y = by_expert(w, xq)
    y = relu2(y + np.repeat(f64(b), C, axis=1))
    return y.reshape(N, E, R, C // R).transpose(0, 2, 1, 3).reshape(N, E * C)

@@ -1,0 +1,178 @@
+from contextlib import ExitStack
+
+import concourse.mybir as mybir
+
+K, T, E, C, N, R = 1024, 1024, 8, 256, 512, 8
+U = C // R
+P = 128
+FLOPS = 2 * E * C * K * N
+
+F32 = mybir.dt.float32
+BF16 = mybir.dt.bfloat16
+I32 = mybir.dt.int32
+U32 = mybir.dt.uint32
+U16 = mybir.dt.uint16
+U8 = mybir.dt.uint8
+FP8X4 = mybir.dt.float8_e4m3fn_x4
+FP4X4 = mybir.dt.float4_e2m1fn_x4
+RELU = mybir.ActivationFunctionType.Relu
+SQUARE = mybir.ActivationFunctionType.Square
+MULT = mybir.AluOpType.mult
+ADD = mybir.AluOpType.add
+MAX = mybir.AluOpType.max
+
+
+def tile_moe_eps_lin_relu2_kernel(tc, xT, w_words, w_scales, b, offs, out):
+    nc = tc.nc
+    with ExitStack() as ctx:
+        keep = ctx.enter_context(tc.tile_pool(name="keep", bufs=1))
+        psum = ctx.enter_context(tc.psum_pool(name="psum", bufs=8))
+
+        offsets = keep.tile([P, E * C // 16], U16, name="offsets")
+        raw = [[keep.tile([P, 4, 512], F32, name=f"raw{a}{c}") for c in range(2)] for a in range(2)]
+        grouped = [[keep.tile([P, 512, 4], BF16, align_bytes=64, name=f"grouped{a}{c}") for c in range(2)] for a in range(2)]
+        words = [keep.tile([P, T], U32, align_bytes=64, name=f"words{a}") for a in range(2)]
+        scales = keep.tile([P, T], U8, align_bytes=64, name="scales")
+        slot_words = [keep.tile([P, E * C], U32, align_bytes=64, name=f"slot_words{a}") for a in range(2)]
+        slot_scales = [keep.tile([P, E * C], U8, align_bytes=64, name=f"slot_scales{a}") for a in range(2)]
+        ww = keep.tile([P, E * 2, 2 * N], U8, align_bytes=64, name="ww")
+        ws = keep.tile([P, E * 2, N], U8, align_bytes=64, name="ws")
+        bias = keep.tile([P, N // P, E], F32, name="bias")
+        results = [keep.tile([P, R, E, U], F32, name=f"results{t}") for t in range(4)]
+
+        def load_x(a, c):
+            rows = xT[512 * a : 512 * (a + 1), 512 * c : 512 * (c + 1)]
+            nc.sync.dma_start(raw[a][c][:], rows.rearrange("(p j) w -> p j w", j=4))
+
+        nc.gpsimd.memset(scales[:], 0)
+        nc.gpsimd.memset(ws[:].bitcast(I32), 0)
+        nc.gpsimd.memset(slot_scales[1][:].bitcast(I32), 0)
+
+        load_x(0, 0)
+        load_x(0, 1)
+        nc.sync.dma_start(offsets[:], offs)
+        load_x(1, 0)
+        load_x(1, 1)
+        nc.sync.dma_start(bias[:], b.rearrange("(t p) e -> p t e", p=P))
+        scale_rows = w_scales.bitcast(I32).rearrange("e a (q r) n -> r q (e a) n", r=4)
+        for r in range(4):
+            nc.sync.dma_start(ws[r:P:32, :, :].bitcast(I32), scale_rows[r])
+        word_rows = w_words.bitcast(I32).rearrange("e a p n -> p (e a) n")
+        for h in range(2):
+            nc.sync.dma_start(ww[:, 8 * h : 8 * h + 8, :].bitcast(I32), word_rows[:, 8 * h : 8 * h + 8, :])
+
+        def interleave(copy, a, c, lo, hi):
+            copy(
+                out=grouped[a][c][:, lo:hi, :].rearrange("p (g i) j -> p g j i", i=4),
+                in_=raw[a][c][:, :, lo:hi].rearrange("p j (g i) -> p g j i", i=4),
+            )
+
+        def quantize(a, c):
+            cols = slice(512 * c, 512 * (c + 1))
+            nc.vector.quantize_mx(
+                out=words[a][:, cols].bitcast(FP8X4),
+                scales=scales[4 * a : P, cols],
+                in_=grouped[a][c][:].rearrange("p w j -> p (w j)"),
+            )
+
+        def gather_words(a, lo, hi):
+            nc.vector.tensor_copy(slot_words[a][:, lo:hi], words[a][:].indirect(offsets[:, lo // 16 : hi // 16]))
+
+        def gather_scales(lo, hi):
+            nc.vector.tensor_copy(slot_scales[0][:, lo:hi], scales[:].indirect(offsets[:, lo // 16 : hi // 16]))
+
+        def move_scales(queue, lo, hi):
+            queue.dma_start(slot_scales[1][: P - 4, lo:hi].bitcast(I32), slot_scales[0][4:P, lo:hi].bitcast(I32))
+
+        def multiply(e0, t):
+            bank = psum.tile([P, 2, C], F32, name="bank")
+            for i in range(2):
+                e = e0 + i
+                for h in range(2):
+                    cols = slice(C * e + P * h, C * e + P * (h + 1))
+                    for a in range(2):
+                        nc.tensor.matmul_mx(
+                            out=bank[:, i, P * h : P * (h + 1)],
+                            lhsT=ww[:, 2 * e + a, 2 * P * t : 2 * P * (t + 1)].bitcast(FP4X4),
+                            lhsT_scale=ws[:, 2 * e + a, P * t : P * (t + 1)],
+                            rhs=slot_words[a][:, cols].bitcast(FP8X4),
+                            rhs_scale=slot_scales[a][:, cols],
+                            start=(a == 0),
+                            stop=(a == 1),
+                        )
+            return bank
+
+        def relu(engine, bank, e, t):
+            sums = bank[:, e % 2, :].rearrange("p (m u) -> p m u", u=U)
+            if engine == "s":
+                nc.scalar.activation(results[t][:, :, e, :], sums, RELU, bias=bias[:, t, e : e + 1])
+            else:
+                nc.vector.tensor_scalar(results[t][:, :, e, :], sums, bias[:, t, e : e + 1], 0.0, ADD, MAX)
+
+        def square(engine, g, t, ranks):
+            v = results[t][:, ranks, 4 * g : 4 * g + 4, :].rearrange("p m e u -> p m (e u)")
+            if engine == "s":
+                nc.scalar.activation(v, v, SQUARE)
+            else:
+                nc.vector.tensor_tensor(v, v, v, MULT)
+
+        def store(t, ranks, lo, hi):
+            rows = out[P * t : P * (t + 1), :].rearrange("p (m e u) -> p m e u", m=R, e=E)
+            nc.sync.dma_start(rows[:, ranks, lo:hi, :], results[t][:, ranks, lo:hi, :])
+
+        for c in range(2):
+            interleave(nc.vector.tensor_copy, 0, c, 0, 384)
+            interleave(nc.scalar.copy, 0, c, 384, 512)
+            quantize(0, c)
+        interleave(nc.scalar.copy, 1, 0, 0, 512)
+        interleave(nc.scalar.copy, 1, 1, 128, 512)
+        interleave(nc.vector.tensor_copy, 1, 1, 0, 128)
+        gather_words(0, 0, 512)
+        gather_words(0, 512, 1024)
+        quantize(1, 0)
+        quantize(1, 1)
+        gather_scales(0, 512)
+        move_scales(nc.scalar, 0, 512)
+        gather_scales(512, 1024)
+        move_scales(nc.scalar, 512, 1024)
+        warm = psum.tile([P, 2, C], F32, name="bank")
+        for i in range(12):
+            nc.tensor.matmul_mx(
+                out=warm[:, 0, :P],
+                lhsT=ww[:, 0, : 2 * P].bitcast(FP4X4),
+                lhsT_scale=ws[:, 0, :P],
+                rhs=slot_words[0][:, :P].bitcast(FP8X4),
+                rhs_scale=slot_scales[0][:, :P],
+                start=True,
+                stop=True,
+            )
+        gather_words(1, 0, 512)
+        gather_words(1, 512, 1024)
+        gather_words(0, 1024, 1536)
+        gather_words(0, 1536, 2048)
+        gather_scales(1024, 1536)
+        move_scales(nc.sync, 1024, 1536)
+        gather_scales(1536, 2048)
+        move_scales(nc.sync, 1536, 2048)
+        gather_words(1, 1024, 1536)
+        gather_words(1, 1536, 2048)
+        all_ranks = slice(0, R)
+        halves = (slice(0, R // 2), slice(R // 2, R))
+        for t in range(4):
+            for e in (0, 2):
+                bank = multiply(e, t)
+                engine = "s" if e == 0 or t < 2 else "v"
+                relu(engine, bank, e, t)
+                relu(engine, bank, e + 1, t)
+            for ranks in halves if t == 0 else (all_ranks,):
+                square("s" if t < 2 else "v", 0, t, ranks)
+                if t < 3:
+                    store(t, ranks, 0, 4)
+        for t in (3, 0, 1, 2):
+            for e, engine in ((4, "v"), (6, "s")):
+                bank = multiply(e, t)
+                relu(engine, bank, e, t)
+                relu(engine, bank, e + 1, t)
+            for engine, ranks in zip("sv", halves):
+                square(engine, 1, t, ranks)
+                store(t, ranks, 0 if t == 3 else 4, 8)

@@ -5,6 +5,8 @@ import concourse.mybir as mybir
 K, T, E, C, N, R = 1024, 1024, 8, 256, 512, 8
 U = C // R
 P = 128
+HALF = T // 2
+G = 4
 FLOPS = 2 * E * C * K * N
 
 F32 = mybir.dt.float32
@@ -29,150 +31,168 @@ def tile_moe_eps_lin_relu2_kernel(tc, xT, w_words, w_scales, b, offs, out):
         psum = ctx.enter_context(tc.psum_pool(name="psum", bufs=8))
 
         offsets = keep.tile([P, E * C // 16], U16, name="offsets")
-        raw = [[keep.tile([P, 4, 512], F32, name=f"raw{a}{c}") for c in range(2)] for a in range(2)]
-        grouped = [[keep.tile([P, 512, 4], BF16, align_bytes=64, name=f"grouped{a}{c}") for c in range(2)] for a in range(2)]
+        raw = [[keep.tile([P, 4, HALF], F32, align_bytes=64, name=f"raw{h}{a}") for a in range(2)] for h in range(2)]
+        grouped = [[keep.tile([P, HALF, 4], BF16, align_bytes=64, name=f"grouped{h}{a}") for a in range(2)] for h in range(2)]
         words = [keep.tile([P, T], U32, align_bytes=64, name=f"words{a}") for a in range(2)]
         scales = keep.tile([P, T], U8, align_bytes=64, name="scales")
-        slot_words = [keep.tile([P, E * C], U32, align_bytes=64, name=f"slot_words{a}") for a in range(2)]
-        slot_scales = [keep.tile([P, E * C], U8, align_bytes=64, name=f"slot_scales{a}") for a in range(2)]
-        ww = keep.tile([P, E * 2, 2 * N], U8, align_bytes=64, name="ww")
-        ws = keep.tile([P, E * 2, N], U8, align_bytes=64, name="ws")
+        slot_words = [[[keep.tile([P, G * P], U32, align_bytes=64, name=f"slot_words{h}{g}{a}") for a in range(2)] for g in range(2)] for h in range(2)]
+        slot_scales = [[[keep.tile([P, G * P], U8, align_bytes=64, name=f"slot_scales{h}{g}")] for g in range(2)] for h in range(2)]
+        ww = [keep.tile([P, 2 * G, 2 * N], U8, align_bytes=64, name=f"ww{g}") for g in range(2)]
+        ws = [keep.tile([P, 2 * G, N], U8, align_bytes=64, name=f"ws{g}") for g in range(2)]
         bias = keep.tile([P, N // P, E], F32, name="bias")
-        results = [keep.tile([P, R, E, U], F32, name=f"results{t}") for t in range(4)]
+        results = [[[keep.tile([P, R // 2, G, U], F32, name=f"results{h}{g}{t}") for t in range(4)] for g in range(2)] for h in range(2)]
 
-        def load_x(a, c):
-            rows = xT[512 * a : 512 * (a + 1), 512 * c : 512 * (c + 1)]
-            nc.sync.dma_start(raw[a][c][:], rows.rearrange("(p j) w -> p j w", j=4))
+        def load_x(h, a):
+            rows = xT[512 * a : 512 * (a + 1), HALF * h : HALF * (h + 1)]
+            nc.sync.dma_start(raw[h][a][:], rows.rearrange("(p j) w -> p j w", j=4))
 
-        nc.gpsimd.memset(scales[:], 0)
-        nc.gpsimd.memset(ws[:].bitcast(I32), 0)
-        nc.gpsimd.memset(slot_scales[1][:].bitcast(I32), 0)
+        def load_weight_scales(g):
+            rows = w_scales[G * g : G * (g + 1)].bitcast(I32).rearrange("e a (q r) n -> r q (e a) n", r=4)
+            for r in range(4):
+                nc.sync.dma_start(ws[g][r:P:32, :, :].bitcast(I32), rows[r])
+
+        def load_weight_words(g):
+            rows = w_words[G * g : G * (g + 1)].bitcast(I32).rearrange("e a p n -> p (e a) n")
+            nc.sync.dma_start(ww[g][:].bitcast(I32), rows)
+
+        def interleave(copy, h, a, lo, hi):
+            copy(
+                out=grouped[h][a][:, lo:hi, :].rearrange("p (g i) j -> p g j i", i=4),
+                in_=raw[h][a][:, :, lo:hi].rearrange("p j (g i) -> p g j i", i=4),
+            )
+
+        def quantize(h, a):
+            cols = slice(HALF * h, HALF * (h + 1))
+            nc.vector.quantize_mx(
+                out=words[a][:, cols].bitcast(FP8X4),
+                scales=scales[4 * a : P, cols],
+                in_=grouped[h][a][:].rearrange("p w j -> p (w j)"),
+            )
+
+        def gather(target, table, h, e):
+            first = (C * e + P * h) // 16
+            window = table[:, : HALF * (h + 1)]
+            nc.vector.tensor_copy(target[:, P * (e % G) : P * (e % G + 1)], window.indirect(offsets[:, first : first + P // 16]))
+
+        def gather_words(h, g, a):
+            for e in range(G * g, G * (g + 1)):
+                gather(slot_words[h][g][a], words[a], h, e)
+
+        def gather_scales(h, g):
+            for e in range(G * g, G * (g + 1)):
+                gather(slot_scales[h][g][0], scales, h, e)
+
+        def second_plane(h, g, tag):
+            plane = keep.tile([P, G * P], U8, align_bytes=64, name=f"second{h}{g}", tag=tag)
+            nc.gpsimd.memset(plane[:].bitcast(I32), 0)
+            slot_scales[h][g].append(plane)
+
+        def move_scales(h, g, queue):
+            both, second = slot_scales[h][g]
+            queue.dma_start(second[: P - 4, :].bitcast(I32), both[4:P, :].bitcast(I32))
+
+        def product(bank, h, e, t):
+            g, i = divmod(e, G)
+            cols = slice(P * i, P * (i + 1))
+            for a in range(2):
+                nc.tensor.matmul_mx(
+                    out=bank[:, i, :],
+                    lhsT=ww[g][:, 2 * i + a, 2 * P * t : 2 * P * (t + 1)].bitcast(FP4X4),
+                    lhsT_scale=ws[g][:, 2 * i + a, P * t : P * (t + 1)],
+                    rhs=slot_words[h][g][a][:, cols].bitcast(FP8X4),
+                    rhs_scale=slot_scales[h][g][a][:, cols],
+                    start=(a == 0),
+                    stop=(a == 1),
+                )
+
+        def multiply(h, g, by_tile):
+            banks = [psum.tile([P, G, P], F32, name="bank") for t in range(4)]
+            pairs = [(e, t) for e in range(G * g, G * (g + 1)) for t in range(4)]
+            for e, t in sorted(pairs, key=lambda pair: pair[1]) if by_tile else pairs:
+                product(banks[t], h, e, t)
+            return banks
+
+        def relu(engine, bank, target, g, t):
+            for i in range(G):
+                sums = bank[:, i, :].rearrange("p (m u) -> p m u", u=U)
+                column = bias[:, t, G * g + i : G * g + i + 1]
+                if engine == "s":
+                    nc.scalar.activation(target[:, :, i, :], sums, RELU, bias=column)
+                else:
+                    nc.vector.tensor_scalar(target[:, :, i, :], sums, column, 0.0, ADD, MAX)
+
+        def square(engine, source, h, g, t):
+            v = source[:].rearrange("p m e u -> p (m e u)")
+            y = results[h][g][t][:].rearrange("p m e u -> p (m e u)")
+            if engine == "s":
+                nc.scalar.activation(y, v, SQUARE)
+            elif engine == "v":
+                nc.vector.tensor_tensor(y, v, v, MULT)
+            else:
+                nc.gpsimd.tensor_tensor(y, v, v, MULT)
+
+        def store(h, g, t):
+            rows = out[P * t : P * (t + 1), :].rearrange("p (m e u) -> p m e u", m=R, e=E)
+            nc.sync.dma_start(rows[:, 4 * h : 4 * h + 4, G * g : G * (g + 1), :], results[h][g][t][:])
+
+        def finish(banks, h, g, relus, squares):
+            rectified = [keep.tile([P, R // 2, G, U], F32, align_bytes=64, name=f"rectified{h}{g}{t}") for t in range(4)]
+            for t in range(5):
+                if t < 4:
+                    relu(relus[t], banks[t], rectified[t], g, t)
+                if t > 0:
+                    square(squares[t - 1], rectified[t - 1], h, g, t - 1)
+                    store(h, g, t - 1)
+
+        nc.vector.memset(ws[0][:].bitcast(I32), 0)
+        nc.vector.memset(ws[1][:].bitcast(I32), 0)
+        nc.gpsimd.memset(scales[:].bitcast(I32), 0)
+        for h in range(2):
+            for g in range(2):
+                second_plane(h, g, f"second{h}{g}")
 
         load_x(0, 0)
         load_x(0, 1)
         nc.sync.dma_start(offsets[:], offs)
         load_x(1, 0)
-        load_x(1, 1)
+        load_weight_scales(0)
+        load_weight_words(0)
         nc.sync.dma_start(bias[:], b.rearrange("(t p) e -> p t e", p=P))
-        scale_rows = w_scales.bitcast(I32).rearrange("e a (q r) n -> r q (e a) n", r=4)
-        for r in range(4):
-            nc.sync.dma_start(ws[r:P:32, :, :].bitcast(I32), scale_rows[r])
-        word_rows = w_words.bitcast(I32).rearrange("e a p n -> p (e a) n")
-        for h in range(2):
-            nc.sync.dma_start(ww[:, 8 * h : 8 * h + 8, :].bitcast(I32), word_rows[:, 8 * h : 8 * h + 8, :])
+        load_x(1, 1)
+        load_weight_scales(1)
+        load_weight_words(1)
 
-        def interleave(copy, a, c, lo, hi):
-            copy(
-                out=grouped[a][c][:, lo:hi, :].rearrange("p (g i) j -> p g j i", i=4),
-                in_=raw[a][c][:, :, lo:hi].rearrange("p j (g i) -> p g j i", i=4),
-            )
-
-        def quantize(a, c):
-            cols = slice(512 * c, 512 * (c + 1))
-            nc.vector.quantize_mx(
-                out=words[a][:, cols].bitcast(FP8X4),
-                scales=scales[4 * a : P, cols],
-                in_=grouped[a][c][:].rearrange("p w j -> p (w j)"),
-            )
-
-        def gather_words(a, lo, hi):
-            nc.vector.tensor_copy(slot_words[a][:, lo:hi], words[a][:].indirect(offsets[:, lo // 16 : hi // 16]))
-
-        def gather_scales(lo, hi):
-            nc.vector.tensor_copy(slot_scales[0][:, lo:hi], scales[:].indirect(offsets[:, lo // 16 : hi // 16]))
-
-        def move_scales(queue, lo, hi):
-            queue.dma_start(slot_scales[1][: P - 4, lo:hi].bitcast(I32), slot_scales[0][4:P, lo:hi].bitcast(I32))
-
-        def multiply(e0, t):
-            bank = psum.tile([P, 2, C], F32, name="bank")
-            for i in range(2):
-                e = e0 + i
-                for h in range(2):
-                    cols = slice(C * e + P * h, C * e + P * (h + 1))
-                    for a in range(2):
-                        nc.tensor.matmul_mx(
-                            out=bank[:, i, P * h : P * (h + 1)],
-                            lhsT=ww[:, 2 * e + a, 2 * P * t : 2 * P * (t + 1)].bitcast(FP4X4),
-                            lhsT_scale=ws[:, 2 * e + a, P * t : P * (t + 1)],
-                            rhs=slot_words[a][:, cols].bitcast(FP8X4),
-                            rhs_scale=slot_scales[a][:, cols],
-                            start=(a == 0),
-                            stop=(a == 1),
-                        )
-            return bank
-
-        def relu(engine, bank, e, t):
-            sums = bank[:, e % 2, :].rearrange("p (m u) -> p m u", u=U)
-            if engine == "s":
-                nc.scalar.activation(results[t][:, :, e, :], sums, RELU, bias=bias[:, t, e : e + 1])
-            else:
-                nc.vector.tensor_scalar(results[t][:, :, e, :], sums, bias[:, t, e : e + 1], 0.0, ADD, MAX)
-
-        def square(engine, g, t, ranks):
-            v = results[t][:, ranks, 4 * g : 4 * g + 4, :].rearrange("p m e u -> p m (e u)")
-            if engine == "s":
-                nc.scalar.activation(v, v, SQUARE)
-            else:
-                nc.vector.tensor_tensor(v, v, v, MULT)
-
-        def store(t, ranks, lo, hi):
-            rows = out[P * t : P * (t + 1), :].rearrange("p (m e u) -> p m e u", m=R, e=E)
-            nc.sync.dma_start(rows[:, ranks, lo:hi, :], results[t][:, ranks, lo:hi, :])
-
-        for c in range(2):
-            interleave(nc.vector.tensor_copy, 0, c, 0, 384)
-            interleave(nc.scalar.copy, 0, c, 384, 512)
-            quantize(0, c)
+        interleave(nc.vector.tensor_copy, 0, 0, 0, 384)
+        interleave(nc.scalar.copy, 0, 0, 384, 512)
+        quantize(0, 0)
+        gather_words(0, 0, 0)
+        interleave(nc.vector.tensor_copy, 0, 1, 0, 320)
+        interleave(nc.scalar.copy, 0, 1, 320, 512)
+        quantize(0, 1)
+        gather_scales(0, 0)
+        move_scales(0, 0, nc.scalar)
         interleave(nc.scalar.copy, 1, 0, 0, 512)
-        interleave(nc.scalar.copy, 1, 1, 128, 512)
-        interleave(nc.vector.tensor_copy, 1, 1, 0, 128)
-        gather_words(0, 0, 512)
-        gather_words(0, 512, 1024)
-        quantize(1, 0)
+        gather_words(0, 0, 1)
+        banks = multiply(0, 0, True)
+        gather_scales(0, 1)
+        move_scales(0, 1, nc.gpsimd)
+        gather_words(0, 1, 0)
+        gather_words(0, 1, 1)
+        interleave(nc.vector.tensor_copy, 1, 1, 0, 512)
         quantize(1, 1)
-        gather_scales(0, 512)
-        move_scales(nc.scalar, 0, 512)
-        gather_scales(512, 1024)
-        move_scales(nc.scalar, 512, 1024)
-        warm = psum.tile([P, 2, C], F32, name="bank")
-        for i in range(12):
-            nc.tensor.matmul_mx(
-                out=warm[:, 0, :P],
-                lhsT=ww[:, 0, : 2 * P].bitcast(FP4X4),
-                lhsT_scale=ws[:, 0, :P],
-                rhs=slot_words[0][:, :P].bitcast(FP8X4),
-                rhs_scale=slot_scales[0][:, :P],
-                start=True,
-                stop=True,
-            )
-        gather_words(1, 0, 512)
-        gather_words(1, 512, 1024)
-        gather_words(0, 1024, 1536)
-        gather_words(0, 1536, 2048)
-        gather_scales(1024, 1536)
-        move_scales(nc.sync, 1024, 1536)
-        gather_scales(1536, 2048)
-        move_scales(nc.sync, 1536, 2048)
-        gather_words(1, 1024, 1536)
-        gather_words(1, 1536, 2048)
-        all_ranks = slice(0, R)
-        halves = (slice(0, R // 2), slice(R // 2, R))
-        for t in range(4):
-            for e in (0, 2):
-                bank = multiply(e, t)
-                engine = "s" if e == 0 or t < 2 else "v"
-                relu(engine, bank, e, t)
-                relu(engine, bank, e + 1, t)
-            for ranks in halves if t == 0 else (all_ranks,):
-                square("s" if t < 2 else "v", 0, t, ranks)
-                if t < 3:
-                    store(t, ranks, 0, 4)
-        for t in (3, 0, 1, 2):
-            for e, engine in ((4, "v"), (6, "s")):
-                bank = multiply(e, t)
-                relu(engine, bank, e, t)
-                relu(engine, bank, e + 1, t)
-            for engine, ranks in zip("sv", halves):
-                square(engine, 1, t, ranks)
-                store(t, ranks, 0 if t == 3 else 4, 8)
+        quantize(1, 0)
+        gather_scales(1, 0)
+        move_scales(1, 0, nc.gpsimd)
+        gather_scales(1, 1)
+        move_scales(1, 1, nc.gpsimd)
+        finish(banks, 0, 0, "ssss", "ssss")
+        banks = multiply(0, 1, True)
+        gather_words(1, 0, 0)
+        gather_words(1, 0, 1)
+        finish(banks, 0, 1, "ssss", "ssss")
+        banks = multiply(1, 0, False)
+        gather_words(1, 1, 0)
+        gather_words(1, 1, 1)
+        finish(banks, 1, 0, "sssv", "sssv")
+        banks = multiply(1, 1, False)
+        finish(banks, 1, 1, "vsvs", "vsvs")

@@ -36,22 +36,24 @@ def tile_moe_eps_lin_relu2_kernel(tc, xT, w_words, w_scales, b, offs, out):
         words = [keep.tile([P, T], U32, align_bytes=64, name=f"words{a}") for a in range(2)]
         scales = keep.tile([P, T], U8, align_bytes=64, name="scales")
         slot_words = [[[keep.tile([P, G * P], U32, align_bytes=64, name=f"slot_words{h}{g}{a}") for a in range(2)] for g in range(2)] for h in range(2)]
-        slot_scales = [[[keep.tile([P, G * P], U8, align_bytes=64, name=f"slot_scales{h}{g}")] for g in range(2)] for h in range(2)]
-        ww = [keep.tile([P, 2 * G, 2 * N], U8, align_bytes=64, name=f"ww{g}") for g in range(2)]
-        ws = [keep.tile([P, 2 * G, N], U8, align_bytes=64, name=f"ws{g}") for g in range(2)]
+        slot_scales = [[keep.tile([P, E * P], U8, align_bytes=64, name=f"slot_scales{h}")] for h in range(2)]
+        ww = []
+        ws = []
         bias = keep.tile([P, N // P, E], F32, name="bias")
-        results = [[[keep.tile([P, R // 2, G, U], F32, name=f"results{h}{g}{t}") for t in range(4)] for g in range(2)] for h in range(2)]
+        results = [[keep.tile([P, R // 2, E, U], F32, name=f"results{h}{t}") for t in range(4)] for h in range(2)]
 
         def load_x(h, a):
             rows = xT[512 * a : 512 * (a + 1), HALF * h : HALF * (h + 1)]
             nc.sync.dma_start(raw[h][a][:], rows.rearrange("(p j) w -> p j w", j=4))
 
-        def load_weight_scales(g):
-            rows = w_scales[G * g : G * (g + 1)].bitcast(I32).rearrange("e a (q r) n -> r q (e a) n", r=4)
+        def load_weight_scales(tag):
+            ws.append(keep.tile([P, 2 * E, N], U8, align_bytes=64, name="ws", tag=tag))
+            rows = w_scales.bitcast(I32).rearrange("e a (q r) n -> r q (e a) n", r=4)
             for r in range(4):
-                nc.sync.dma_start(ws[g][r:P:32, :, :].bitcast(I32), rows[r])
+                nc.sync.dma_start(ws[0][r:P:32, :, :].bitcast(I32), rows[r])
 
-        def load_weight_words(g):
+        def load_weight_words(g, tag):
+            ww.append(keep.tile([P, 2 * G, 2 * N], U8, align_bytes=64, name=f"ww{g}", tag=tag))
             rows = w_words[G * g : G * (g + 1)].bitcast(I32).rearrange("e a p n -> p (e a) n")
             nc.sync.dma_start(ww[g][:].bitcast(I32), rows)
 
@@ -72,127 +74,108 @@ def tile_moe_eps_lin_relu2_kernel(tc, xT, w_words, w_scales, b, offs, out):
         def gather(target, table, h, e):
             first = (C * e + P * h) // 16
             window = table[:, : HALF * (h + 1)]
-            nc.vector.tensor_copy(target[:, P * (e % G) : P * (e % G + 1)], window.indirect(offsets[:, first : first + P // 16]))
+            nc.vector.tensor_copy(target, window.indirect(offsets[:, first : first + P // 16]))
 
         def gather_words(h, g, a):
-            for e in range(G * g, G * (g + 1)):
-                gather(slot_words[h][g][a], words[a], h, e)
-
-        def gather_scales(h, g):
-            for e in range(G * g, G * (g + 1)):
-                gather(slot_scales[h][g][0], scales, h, e)
-
-        def second_plane(h, g, tag):
-            plane = keep.tile([P, G * P], U8, align_bytes=64, name=f"second{h}{g}", tag=tag)
-            nc.gpsimd.memset(plane[:].bitcast(I32), 0)
-            slot_scales[h][g].append(plane)
-
-        def move_scales(h, g, queue):
-            both, second = slot_scales[h][g]
-            queue.dma_start(second[: P - 4, :].bitcast(I32), both[4:P, :].bitcast(I32))
-
-        def product(bank, h, e, t):
-            g, i = divmod(e, G)
-            cols = slice(P * i, P * (i + 1))
-            for a in range(2):
-                nc.tensor.matmul_mx(
-                    out=bank[:, i, :],
-                    lhsT=ww[g][:, 2 * i + a, 2 * P * t : 2 * P * (t + 1)].bitcast(FP4X4),
-                    lhsT_scale=ws[g][:, 2 * i + a, P * t : P * (t + 1)],
-                    rhs=slot_words[h][g][a][:, cols].bitcast(FP8X4),
-                    rhs_scale=slot_scales[h][g][a][:, cols],
-                    start=(a == 0),
-                    stop=(a == 1),
-                )
-
-        def multiply(h, g, by_tile):
-            banks = [psum.tile([P, G, P], F32, name="bank") for t in range(4)]
-            pairs = [(e, t) for e in range(G * g, G * (g + 1)) for t in range(4)]
-            for e, t in sorted(pairs, key=lambda pair: pair[1]) if by_tile else pairs:
-                product(banks[t], h, e, t)
-            return banks
-
-        def relu(engine, bank, target, g, t):
             for i in range(G):
+                gather(slot_words[h][g][a][:, P * i : P * (i + 1)], words[a], h, G * g + i)
+
+        def gather_scales(h):
+            for e in range(E):
+                gather(slot_scales[h][0][:, P * e : P * (e + 1)], scales, h, e)
+
+        def second_plane(h, tag):
+            plane = keep.tile([P, E * P], U8, align_bytes=64, name=f"second{h}", tag=tag)
+            slot_scales[h].append(plane)
+
+        def move_scales(h, queue):
+            both, second = slot_scales[h]
+            for lo, count in ((0, 64), (64, 32), (96, 4)):
+                queue.dma_start(second[lo : lo + count, :].bitcast(I32), both[lo + 4 : lo + 4 + count, :].bitcast(I32))
+
+        def multiply(h, g, t):
+            bank = psum.tile([P, G, P], F32, name="bank")
+            for i in range(G):
+                e = G * g + i
+                for a in range(2):
+                    nc.tensor.matmul_mx(
+                        out=bank[:, i, :],
+                        lhsT=ww[g][:, 2 * i + a, 2 * P * t : 2 * P * (t + 1)].bitcast(FP4X4),
+                        lhsT_scale=ws[0][:, 2 * e + a, P * t : P * (t + 1)],
+                        rhs=slot_words[h][g][a][:, P * i : P * (i + 1)].bitcast(FP8X4),
+                        rhs_scale=slot_scales[h][a][:, P * e : P * (e + 1)],
+                        start=(a == 0),
+                        stop=(a == 1),
+                    )
+            return bank
+
+        def relu(engine, bank, h, g, t):
+            for i in range(G):
+                e = G * g + i
                 sums = bank[:, i, :].rearrange("p (m u) -> p m u", u=U)
-                column = bias[:, t, G * g + i : G * g + i + 1]
                 if engine == "s":
-                    nc.scalar.activation(target[:, :, i, :], sums, RELU, bias=column)
+                    nc.scalar.activation(results[h][t][:, :, e, :], sums, RELU, bias=bias[:, t, e : e + 1])
                 else:
-                    nc.vector.tensor_scalar(target[:, :, i, :], sums, column, 0.0, ADD, MAX)
+                    nc.vector.tensor_scalar(results[h][t][:, :, e, :], sums, bias[:, t, e : e + 1], 0.0, ADD, MAX)
 
-        def square(engine, source, h, g, t):
-            v = source[:].rearrange("p m e u -> p (m e u)")
-            y = results[h][g][t][:].rearrange("p m e u -> p (m e u)")
+        def square(engine, h, g, t):
+            v = results[h][t][:, :, G * g : G * (g + 1), :].rearrange("p m e u -> p m (e u)")
             if engine == "s":
-                nc.scalar.activation(y, v, SQUARE)
+                nc.scalar.activation(v, v, SQUARE)
             elif engine == "v":
-                nc.vector.tensor_tensor(y, v, v, MULT)
+                nc.vector.tensor_tensor(v, v, v, MULT)
             else:
-                nc.gpsimd.tensor_tensor(y, v, v, MULT)
+                nc.gpsimd.tensor_tensor(v, v, v, MULT)
 
-        def store(h, g, t):
-            rows = out[P * t : P * (t + 1), :].rearrange("p (m e u) -> p m e u", m=R, e=E)
-            nc.sync.dma_start(rows[:, 4 * h : 4 * h + 4, G * g : G * (g + 1), :], results[h][g][t][:])
+        def store(h, t):
+            rows = out[P * t : P * (t + 1), T * h : T * (h + 1)]
+            nc.sync.dma_start(rows, results[h][t][:].rearrange("p m e u -> p (m e u)"))
 
-        def finish(banks, h, g, relus, squares):
-            rectified = [keep.tile([P, R // 2, G, U], F32, align_bytes=64, name=f"rectified{h}{g}{t}") for t in range(4)]
-            for t in range(5):
-                if t < 4:
-                    relu(relus[t], banks[t], rectified[t], g, t)
-                if t > 0:
-                    square(squares[t - 1], rectified[t - 1], h, g, t - 1)
-                    store(h, g, t - 1)
+        def finish(h, steps):
+            done = set()
+            for g, t, engine in steps:
+                relu(engine, multiply(h, g, t), h, g, t)
+                square(engine, h, g, t)
+                if (1 - g, t) in done:
+                    store(h, t)
+                done.add((g, t))
 
-        nc.vector.memset(ws[0][:].bitcast(I32), 0)
-        nc.vector.memset(ws[1][:].bitcast(I32), 0)
         nc.gpsimd.memset(scales[:].bitcast(I32), 0)
-        for h in range(2):
-            for g in range(2):
-                second_plane(h, g, f"second{h}{g}")
+        second_plane(1, "second1")
+        nc.gpsimd.memset(slot_scales[1][1][:].bitcast(I32), 0)
 
+        nc.scalar.dma_start(bias[:], b.rearrange("(t p) e -> p t e", p=P))
         load_x(0, 0)
-        load_x(0, 1)
         nc.sync.dma_start(offsets[:], offs)
+        load_x(0, 1)
         load_x(1, 0)
-        load_weight_scales(0)
-        load_weight_words(0)
-        nc.sync.dma_start(bias[:], b.rearrange("(t p) e -> p t e", p=P))
         load_x(1, 1)
-        load_weight_scales(1)
-        load_weight_words(1)
 
         interleave(nc.vector.tensor_copy, 0, 0, 0, 384)
         interleave(nc.scalar.copy, 0, 0, 384, 512)
+        load_weight_scales("raw00")
         quantize(0, 0)
         gather_words(0, 0, 0)
         interleave(nc.vector.tensor_copy, 0, 1, 0, 320)
         interleave(nc.scalar.copy, 0, 1, 320, 512)
+        load_weight_words(0, "raw01")
         quantize(0, 1)
-        gather_scales(0, 0)
-        move_scales(0, 0, nc.scalar)
+        load_weight_words(1, "grouped01")
+        gather_scales(0)
         interleave(nc.scalar.copy, 1, 0, 0, 512)
+        second_plane(0, "raw10")
+        move_scales(0, nc.scalar)
+        interleave(nc.scalar.copy, 1, 1, 0, 256)
+        interleave(nc.scalar.copy, 1, 1, 256, 512)
         gather_words(0, 0, 1)
-        banks = multiply(0, 0, True)
-        gather_scales(0, 1)
-        move_scales(0, 1, nc.gpsimd)
         gather_words(0, 1, 0)
         gather_words(0, 1, 1)
-        interleave(nc.vector.tensor_copy, 1, 1, 0, 512)
         quantize(1, 1)
         quantize(1, 0)
-        gather_scales(1, 0)
-        move_scales(1, 0, nc.gpsimd)
-        gather_scales(1, 1)
-        move_scales(1, 1, nc.gpsimd)
-        finish(banks, 0, 0, "ssss", "ssss")
-        banks = multiply(0, 1, True)
-        gather_words(1, 0, 0)
-        gather_words(1, 0, 1)
-        finish(banks, 0, 1, "ssss", "ssss")
-        banks = multiply(1, 0, False)
-        gather_words(1, 1, 0)
-        gather_words(1, 1, 1)
-        finish(banks, 1, 0, "sssv", "sssv")
-        banks = multiply(1, 1, False)
-        finish(banks, 1, 1, "vsvs", "vsvs")
+        gather_scales(1)
+        move_scales(1, nc.sync)
+        for g in range(2):
+            for a in range(2):
+                gather_words(1, g, a)
+        finish(0, [(0, 0, "s"), (0, 1, "s"), (0, 2, "s"), (1, 0, "s"), (1, 1, "s"), (1, 2, "s"), (0, 3, "s"), (1, 3, "s")])
+        finish(1, [(0, 0, "v"), (1, 0, "v"), (0, 1, "s"), (1, 1, "s"), (0, 2, "v"), (1, 2, "v"), (0, 3, "s"), (1, 3, "v")])

@@ -35,7 +35,7 @@ def tile_moe_eps_lin_relu2_kernel(tc, xT, w_words, w_scales, b, offs, out):
         grouped = [[keep.tile([P, HALF, 4], BF16, align_bytes=64, name=f"grouped{h}{a}") for a in range(2)] for h in range(2)]
         words = [keep.tile([P, T], U32, align_bytes=64, name=f"words{a}") for a in range(2)]
         scales = keep.tile([P, T], U8, align_bytes=64, name="scales")
-        slot_words = [[[keep.tile([P, G * P], U32, align_bytes=64, name=f"slot_words{h}{g}{a}") for a in range(2)] for g in range(2)] for h in range(2)]
+        slot_words = {}
         slot_scales = [[keep.tile([P, E * P], U8, align_bytes=64, name=f"slot_scales{h}")] for h in range(2)]
         ww = []
         ws = []
@@ -76,9 +76,11 @@ def tile_moe_eps_lin_relu2_kernel(tc, xT, w_words, w_scales, b, offs, out):
             window = table[:, : HALF * (h + 1)]
             nc.vector.tensor_copy(target, window.indirect(offsets[:, first : first + P // 16]))
 
-        def gather_words(h, g, a):
+        def gather_words(h, g, a, tag=None):
+            name = f"slot_words{h}{g}{a}"
+            slot_words[h, g, a] = keep.tile([P, G * P], U32, align_bytes=64, name=name, tag=tag or name)
             for i in range(G):
-                gather(slot_words[h][g][a][:, P * i : P * (i + 1)], words[a], h, G * g + i)
+                gather(slot_words[h, g, a][:, P * i : P * (i + 1)], words[a], h, G * g + i)
 
         def gather_scales(h):
             for e in range(E):
@@ -102,7 +104,7 @@ def tile_moe_eps_lin_relu2_kernel(tc, xT, w_words, w_scales, b, offs, out):
                         out=bank[:, i, :],
                         lhsT=ww[g][:, 2 * i + a, 2 * P * t : 2 * P * (t + 1)].bitcast(FP4X4),
                         lhsT_scale=ws[0][:, 2 * e + a, P * t : P * (t + 1)],
-                        rhs=slot_words[h][g][a][:, P * i : P * (i + 1)].bitcast(FP8X4),
+                        rhs=slot_words[h, g, a][:, P * i : P * (i + 1)].bitcast(FP8X4),
                         rhs_scale=slot_scales[h][a][:, P * e : P * (e + 1)],
                         start=(a == 0),
                         stop=(a == 1),
@@ -110,20 +112,23 @@ def tile_moe_eps_lin_relu2_kernel(tc, xT, w_words, w_scales, b, offs, out):
             return bank
 
         def relu(engine, bank, h, g, t):
-            for i in range(G):
-                e = G * g + i
-                sums = bank[:, i, :].rearrange("p (m u) -> p m u", u=U)
-                if engine == "s":
+            if engine == "s":
+                for i in range(G):
+                    e = G * g + i
+                    sums = bank[:, i, :].rearrange("p (m u) -> p m u", u=U)
                     nc.scalar.activation(results[h][t][:, :, e, :], sums, RELU, bias=bias[:, t, e : e + 1])
-                else:
-                    nc.vector.tensor_scalar(results[h][t][:, :, e, :], sums, bias[:, t, e : e + 1], 0.0, ADD, MAX)
+            else:
+                target = results[h][t][:, :, G * g : G * (g + 1), :].rearrange("p m e u -> p e m u")
+                sums = bank[:].rearrange("p e (m u) -> p e m u", u=U)
+                spread = bias[:, t, G * g : G * (g + 1)].unsqueeze(2).unsqueeze(3).to_broadcast([P, G, R // 2, U])
+                nc.vector.tensor_tensor(target, sums, spread, ADD)
 
         def square(engine, h, g, t):
             v = results[h][t][:, :, G * g : G * (g + 1), :].rearrange("p m e u -> p m (e u)")
             if engine == "s":
                 nc.scalar.activation(v, v, SQUARE)
             elif engine == "v":
-                nc.vector.tensor_tensor(v, v, v, MULT)
+                nc.vector.scalar_tensor_tensor(v, v, 0.0, v, MAX, MULT)
             else:
                 nc.gpsimd.tensor_tensor(v, v, v, MULT)
 
@@ -133,16 +138,18 @@ def tile_moe_eps_lin_relu2_kernel(tc, xT, w_words, w_scales, b, offs, out):
 
         def finish(h, steps):
             done = set()
-            for g, t, engine in steps:
-                relu(engine, multiply(h, g, t), h, g, t)
-                square(engine, h, g, t)
+            for g, t, engines in steps:
+                relu(engines[0], multiply(h, g, t), h, g, t)
+                square(engines[1], h, g, t)
                 if (1 - g, t) in done:
                     store(h, t)
                 done.add((g, t))
 
         nc.gpsimd.memset(scales[:].bitcast(I32), 0)
         second_plane(1, "second1")
-        nc.gpsimd.memset(slot_scales[1][1][:].bitcast(I32), 0)
+        warm = keep.tile([P, 8], F32, name="warm")
+        nc.gpsimd.memset(warm[:], 0.0)
+        nc.gpsimd.tensor_tensor(warm[:], warm[:], warm[:], MULT)
 
         nc.scalar.dma_start(bias[:], b.rearrange("(t p) e -> p t e", p=P))
         load_x(0, 0)
@@ -160,15 +167,15 @@ def tile_moe_eps_lin_relu2_kernel(tc, xT, w_words, w_scales, b, offs, out):
         interleave(nc.scalar.copy, 0, 1, 320, 512)
         load_weight_words(0, "raw01")
         quantize(0, 1)
-        load_weight_words(1, "grouped01")
         gather_scales(0)
         interleave(nc.scalar.copy, 1, 0, 0, 512)
         second_plane(0, "raw10")
         move_scales(0, nc.scalar)
         interleave(nc.scalar.copy, 1, 1, 0, 256)
         interleave(nc.scalar.copy, 1, 1, 256, 512)
+        load_weight_words(1, "raw11")
         gather_words(0, 0, 1)
-        gather_words(0, 1, 0)
+        gather_words(0, 1, 0, "grouped01")
         gather_words(0, 1, 1)
         quantize(1, 1)
         quantize(1, 0)
@@ -177,5 +184,5 @@ def tile_moe_eps_lin_relu2_kernel(tc, xT, w_words, w_scales, b, offs, out):
         for g in range(2):
             for a in range(2):
                 gather_words(1, g, a)
-        finish(0, [(0, 0, "s"), (0, 1, "s"), (0, 2, "s"), (1, 0, "s"), (1, 1, "s"), (1, 2, "s"), (0, 3, "s"), (1, 3, "s")])
-        finish(1, [(0, 0, "v"), (1, 0, "v"), (0, 1, "s"), (1, 1, "s"), (0, 2, "v"), (1, 2, "v"), (0, 3, "s"), (1, 3, "v")])
+        finish(0, [(0, 0, "sg"), (0, 1, "sg"), (0, 2, "sg"), (1, 0, "sg"), (1, 1, "sg"), (1, 2, "sg"), (0, 3, "ss"), (1, 3, "ss")])
+        finish(1, [(0, 0, "ss"), (0, 1, "ss"), (1, 0, "vv"), (1, 1, "ss"), (0, 2, "ss"), (1, 2, "vv"), (0, 3, "ss"), (1, 3, "vv")])

@@ -50,7 +50,7 @@ def tile_moe_eps_lin_relu2_kernel(tc, xT, w_words, w_scales, b, offs, out):
             ws.append(keep.tile([P, 2 * E, N], U8, align_bytes=64, name="ws", tag=tag))
             rows = w_scales.bitcast(I32).rearrange("e a (q r) n -> r q (e a) n", r=4)
             for r in range(4):
-                nc.sync.dma_start(ws[0][r:P:32, :, :].bitcast(I32), rows[r])
+                nc.gpsimd.dma_start(ws[0][r:P:32, :, :].bitcast(I32), rows[r])
 
         def load_weight_words(g, tag):
             ww.append(keep.tile([P, 2 * G, 2 * N], U8, align_bytes=64, name=f"ww{g}", tag=tag))
@@ -147,10 +147,8 @@ def tile_moe_eps_lin_relu2_kernel(tc, xT, w_words, w_scales, b, offs, out):
 
         nc.gpsimd.memset(scales[:].bitcast(I32), 0)
         second_plane(1, "second1")
-        warm = keep.tile([P, 8], F32, name="warm")
-        nc.gpsimd.memset(warm[:], 0.0)
-        nc.gpsimd.tensor_tensor(warm[:], warm[:], warm[:], MULT)
 
+        load_weight_scales("ws")
         nc.scalar.dma_start(bias[:], b.rearrange("(t p) e -> p t e", p=P))
         load_x(0, 0)
         nc.sync.dma_start(offsets[:], offs)
@@ -160,7 +158,6 @@ def tile_moe_eps_lin_relu2_kernel(tc, xT, w_words, w_scales, b, offs, out):
 
         interleave(nc.vector.tensor_copy, 0, 0, 0, 384)
         interleave(nc.scalar.copy, 0, 0, 384, 512)
-        load_weight_scales("raw00")
         quantize(0, 0)
         gather_words(0, 0, 0)
         interleave(nc.vector.tensor_copy, 0, 1, 0, 320)

@@ -40,7 +40,7 @@ def tile_moe_eps_lin_relu2_kernel(tc, xT, w_words, w_scales, b, offs, out):
         ww = []
         ws = []
         bias = keep.tile([P, N // P, E], F32, name="bias")
-        results = [[keep.tile([P, R // 2, E, U], F32, name=f"results{h}{t}") for t in range(4)] for h in range(2)]
+        results = [keep.tile([P, 4, R // 2, E, U], F32, name=f"results{h}") for h in range(2)]
 
         def load_x(h, a):
             rows = xT[512 * a : 512 * (a + 1), HALF * h : HALF * (h + 1)]
@@ -76,55 +76,45 @@ def tile_moe_eps_lin_relu2_kernel(tc, xT, w_words, w_scales, b, offs, out):
             window = table[:, : HALF * (h + 1)]
             nc.vector.tensor_copy(target, window.indirect(offsets[:, first : first + P // 16]))
 
-        def gather_words(h, g, a, tag=None):
-            name = f"slot_words{h}{g}{a}"
-            slot_words[h, g, a] = keep.tile([P, G * P], U32, align_bytes=64, name=name, tag=tag or name)
-            for i in range(G):
-                gather(slot_words[h, g, a][:, P * i : P * (i + 1)], words[a], h, G * g + i)
+        def gather_words(h, experts, a, tag=None):
+            name = f"slot_words{h}{experts[0]}{a}"
+            tile = keep.tile([P, len(experts) * P], U32, align_bytes=64, name=name, tag=tag or name)
+            for i, e in enumerate(experts):
+                slot_words[h, e, a] = tile[:, P * i : P * (i + 1)]
+                gather(slot_words[h, e, a], words[a], h, e)
 
-        def gather_scales(h):
-            for e in range(E):
+        def gather_scales(h, experts):
+            for e in experts:
                 gather(slot_scales[h][0][:, P * e : P * (e + 1)], scales, h, e)
 
         def second_plane(h, tag):
             plane = keep.tile([P, E * P], U8, align_bytes=64, name=f"second{h}", tag=tag)
             slot_scales[h].append(plane)
 
-        def move_scales(h, queue):
+        def move_scales(h, queue, experts):
             both, second = slot_scales[h]
+            cols = slice(P * experts[0], P * (experts[-1] + 1))
             for lo, count in ((0, 64), (64, 32), (96, 4)):
-                queue.dma_start(second[lo : lo + count, :].bitcast(I32), both[lo + 4 : lo + 4 + count, :].bitcast(I32))
+                queue.dma_start(second[lo : lo + count, cols].bitcast(I32), both[lo + 4 : lo + 4 + count, cols].bitcast(I32))
 
-        def multiply(h, g, t):
-            bank = psum.tile([P, G, P], F32, name="bank")
-            for i in range(G):
-                e = G * g + i
-                for a in range(2):
-                    nc.tensor.matmul_mx(
-                        out=bank[:, i, :],
-                        lhsT=ww[g][:, 2 * i + a, 2 * P * t : 2 * P * (t + 1)].bitcast(FP4X4),
-                        lhsT_scale=ws[0][:, 2 * e + a, P * t : P * (t + 1)],
-                        rhs=slot_words[h, g, a][:, P * i : P * (i + 1)].bitcast(FP8X4),
-                        rhs_scale=slot_scales[h][a][:, P * e : P * (e + 1)],
-                        start=(a == 0),
-                        stop=(a == 1),
-                    )
-            return bank
+        def product(target, h, e, t):
+            g, i = divmod(e, G)
+            for a in range(2):
+                nc.tensor.matmul_mx(
+                    out=target,
+                    lhsT=ww[g][:, 2 * i + a, 2 * P * t : 2 * P * (t + 1)].bitcast(FP4X4),
+                    lhsT_scale=ws[0][:, 2 * e + a, P * t : P * (t + 1)],
+                    rhs=slot_words[h, e, a].bitcast(FP8X4),
+                    rhs_scale=slot_scales[h][a][:, P * e : P * (e + 1)],
+                    start=(a == 0),
+                    stop=(a == 1),
+                )
 
-        def relu(engine, bank, h, g, t):
-            if engine == "s":
-                for i in range(G):
-                    e = G * g + i
-                    sums = bank[:, i, :].rearrange("p (m u) -> p m u", u=U)
-                    nc.scalar.activation(results[h][t][:, :, e, :], sums, RELU, bias=bias[:, t, e : e + 1])
-            else:
-                target = results[h][t][:, :, G * g : G * (g + 1), :].rearrange("p m e u -> p e m u")
-                sums = bank[:].rearrange("p e (m u) -> p e m u", u=U)
-                spread = bias[:, t, G * g : G * (g + 1)].unsqueeze(2).unsqueeze(3).to_broadcast([P, G, R // 2, U])
-                nc.vector.tensor_tensor(target, sums, spread, ADD)
+        def rectify(sums, h, e, t):
+            nc.scalar.activation(results[h][:, t, :, e, :], sums.rearrange("p (m u) -> p m u", u=U), RELU, bias=bias[:, t, e : e + 1])
 
-        def square(engine, h, g, t):
-            v = results[h][t][:, :, G * g : G * (g + 1), :].rearrange("p m e u -> p m (e u)")
+        def square(engine, h, tiles, experts):
+            v = results[h][:, tiles, :, experts, :].rearrange("p t m e u -> p (t m) (e u)")
             if engine == "s":
                 nc.scalar.activation(v, v, SQUARE)
             elif engine == "v":
@@ -134,18 +124,30 @@ def tile_moe_eps_lin_relu2_kernel(tc, xT, w_words, w_scales, b, offs, out):
 
         def store(h, t):
             rows = out[P * t : P * (t + 1), T * h : T * (h + 1)]
-            nc.sync.dma_start(rows, results[h][t][:].rearrange("p m e u -> p (m e u)"))
+            nc.sync.dma_start(rows, results[h][:, t].rearrange("p m e u -> p (m e u)"))
 
-        def finish(h, steps):
-            done = set()
-            for g, t, engines in steps:
-                relu(engines[0], multiply(h, g, t), h, g, t)
-                square(engines[1], h, g, t)
-                if (1 - g, t) in done:
-                    store(h, t)
-                done.add((g, t))
+        def by_tile(h, g, t):
+            bank = psum.tile([P, G, P], F32, name="bank")
+            for i in range(G):
+                product(bank[:, i, :], h, G * g + i, t)
+            for i in range(G):
+                rectify(bank[:, i, :], h, G * g + i, t)
 
+        def by_expert(h, e, engine):
+            bank = psum.tile([P, 4, P], F32, name="bank")
+            for t in range(4):
+                product(bank[:, t, :], h, e, t)
+            if engine == "s":
+                for t in range(4):
+                    rectify(bank[:, t, :], h, e, t)
+            else:
+                sums = bank[:].rearrange("p t (m u) -> p t m u", u=U)
+                spread = bias[:, :, e].unsqueeze(2).unsqueeze(3).to_broadcast([P, 4, R // 2, U])
+                nc.vector.tensor_tensor(results[h][:, :, :, e, :], sums, spread, ADD)
+
+        low, high = range(G), range(G, E)
         nc.gpsimd.memset(scales[:].bitcast(I32), 0)
+        second_plane(0, "second0")
         second_plane(1, "second1")
 
         load_weight_scales("ws")
@@ -158,28 +160,38 @@ def tile_moe_eps_lin_relu2_kernel(tc, xT, w_words, w_scales, b, offs, out):
 
         interleave(nc.vector.tensor_copy, 0, 0, 0, 384)
         interleave(nc.scalar.copy, 0, 0, 384, 512)
+        load_weight_words(0, "raw00")
         quantize(0, 0)
-        gather_words(0, 0, 0)
-        interleave(nc.vector.tensor_copy, 0, 1, 0, 320)
-        interleave(nc.scalar.copy, 0, 1, 320, 512)
-        load_weight_words(0, "raw01")
+        gather_words(0, range(E), 0)
+        interleave(nc.scalar.copy, 0, 1, 0, 512)
         quantize(0, 1)
-        gather_scales(0)
+        for experts in (low, high):
+            gather_scales(0, experts)
+            move_scales(0, nc.sync, experts)
         interleave(nc.scalar.copy, 1, 0, 0, 512)
-        second_plane(0, "raw10")
-        move_scales(0, nc.scalar)
-        interleave(nc.scalar.copy, 1, 1, 0, 256)
-        interleave(nc.scalar.copy, 1, 1, 256, 512)
-        load_weight_words(1, "raw11")
-        gather_words(0, 0, 1)
-        gather_words(0, 1, 0, "grouped01")
-        gather_words(0, 1, 1)
+        load_weight_words(1, "raw10")
+        interleave(nc.scalar.copy, 1, 1, 0, 512)
+        gather_words(0, low, 1)
+        gather_words(0, high, 1)
         quantize(1, 1)
         quantize(1, 0)
-        gather_scales(1)
-        move_scales(1, nc.sync)
-        for g in range(2):
+        for experts in (low, high):
+            gather_scales(1, experts)
+            move_scales(1, nc.sync, experts)
+        for e in range(E):
             for a in range(2):
-                gather_words(1, g, a)
-        finish(0, [(0, 0, "sg"), (0, 1, "sg"), (0, 2, "sg"), (1, 0, "sg"), (1, 1, "sg"), (1, 2, "sg"), (0, 3, "ss"), (1, 3, "ss")])
-        finish(1, [(0, 0, "ss"), (0, 1, "ss"), (1, 0, "vv"), (1, 1, "ss"), (0, 2, "ss"), (1, 2, "vv"), (0, 3, "ss"), (1, 3, "vv")])
+                gather_words(1, [e], a)
+        for g, engines in enumerate(("gggs", "ggss")):
+            for t in range(4):
+                by_tile(0, g, t)
+                square(engines[t], 0, slice(t, t + 1), slice(G * g, G * (g + 1)))
+                if g == 1:
+                    store(0, t)
+        for e in range(E):
+            by_expert(1, e, "s" if e < 6 else "v")
+            if e < 2:
+                square("g", 1, slice(0, 4), slice(e, e + 1))
+        for t in range(4):
+            square("s", 1, slice(t, t + 1), slice(2, 6))
+            square("v", 1, slice(t, t + 1), slice(6, 8))
+            store(1, t)

@@ -126,24 +126,27 @@ def tile_moe_eps_lin_relu2_kernel(tc, xT, w_words, w_scales, b, offs, out):
             rows = out[P * t : P * (t + 1), T * h : T * (h + 1)]
             nc.sync.dma_start(rows, results[h][:, t].rearrange("p m e u -> p (m e u)"))
 
-        def by_tile(h, g, t):
-            bank = psum.tile([P, G, P], F32, name="bank")
-            for i in range(G):
-                product(bank[:, i, :], h, G * g + i, t)
-            for i in range(G):
-                rectify(bank[:, i, :], h, G * g + i, t)
-
-        def by_expert(h, e, engine):
+        def multiply(h, experts, tiles):
             bank = psum.tile([P, 4, P], F32, name="bank")
-            for t in range(4):
-                product(bank[:, t, :], h, e, t)
-            if engine == "s":
-                for t in range(4):
-                    rectify(bank[:, t, :], h, e, t)
-            else:
-                sums = bank[:].rearrange("p t (m u) -> p t m u", u=U)
-                spread = bias[:, :, e].unsqueeze(2).unsqueeze(3).to_broadcast([P, 4, R // 2, U])
-                nc.vector.tensor_tensor(results[h][:, :, :, e, :], sums, spread, ADD)
+            pairs = [(e, t) for e in experts for t in tiles]
+            for i, (e, t) in enumerate(pairs):
+                product(bank[:, i, :], h, e, t)
+            return bank, pairs
+
+        def rectify_bank(h, bank, pairs):
+            for i, (e, t) in enumerate(pairs):
+                rectify(bank[:, i, :], h, e, t)
+
+        def add_bias_tiles(h, bank, e, count):
+            sums = bank[:, :count, :].rearrange("p t (m u) -> p t m u", u=U)
+            spread = bias[:, :count, e].unsqueeze(2).unsqueeze(3).to_broadcast([P, count, R // 2, U])
+            nc.vector.tensor_tensor(results[h][:, :count, :, e, :], sums, spread, ADD)
+
+        def add_bias_experts(h, bank, g, t):
+            target = results[h][:, t, :, G * g : G * (g + 1), :].rearrange("p m e u -> p e m u")
+            sums = bank[:].rearrange("p e (m u) -> p e m u", u=U)
+            spread = bias[:, t, G * g : G * (g + 1)].unsqueeze(2).unsqueeze(3).to_broadcast([P, G, R // 2, U])
+            nc.vector.tensor_tensor(target, sums, spread, ADD)
 
         low, high = range(G), range(G, E)
         nc.gpsimd.memset(scales[:].bitcast(I32), 0)
@@ -158,12 +161,13 @@ def tile_moe_eps_lin_relu2_kernel(tc, xT, w_words, w_scales, b, offs, out):
         load_x(1, 0)
         load_x(1, 1)
 
-        interleave(nc.vector.tensor_copy, 0, 0, 0, 384)
-        interleave(nc.scalar.copy, 0, 0, 384, 512)
+        interleave(nc.vector.tensor_copy, 0, 0, 0, 352)
+        interleave(nc.scalar.copy, 0, 0, 352, 512)
         load_weight_words(0, "raw00")
         quantize(0, 0)
+        interleave(nc.vector.tensor_copy, 0, 1, 0, 64)
         gather_words(0, range(E), 0)
-        interleave(nc.scalar.copy, 0, 1, 0, 512)
+        interleave(nc.scalar.copy, 0, 1, 64, 512)
         quantize(0, 1)
         for experts in (low, high):
             gather_scales(0, experts)
@@ -181,17 +185,31 @@ def tile_moe_eps_lin_relu2_kernel(tc, xT, w_words, w_scales, b, offs, out):
         for e in range(E):
             for a in range(2):
                 gather_words(1, [e], a)
-        for g, engines in enumerate(("gggs", "ggss")):
+        for g, engines in enumerate(("gggg", "ggss")):
             for t in range(4):
-                by_tile(0, g, t)
+                rectify_bank(0, *multiply(0, (low, high)[g], [t]))
                 square(engines[t], 0, slice(t, t + 1), slice(G * g, G * (g + 1)))
                 if g == 1:
                     store(0, t)
-        for e in range(E):
-            by_expert(1, e, "s" if e < 6 else "v")
-            if e < 2:
-                square("g", 1, slice(0, 4), slice(e, e + 1))
-        for t in range(4):
-            square("s", 1, slice(t, t + 1), slice(2, 6))
-            square("v", 1, slice(t, t + 1), slice(6, 8))
-            store(1, t)
+        later = {}
+        for pair in range(3):
+            rectify_bank(1, *multiply(1, [2 * pair, 2 * pair + 1], [0, 1]))
+            square("ggs"[pair], 1, slice(0, 2), slice(2 * pair, 2 * pair + 2))
+            if pair == 1:
+                later[0, 2] = multiply(1, low, [2])
+        for e in (6, 7):
+            add_bias_tiles(1, multiply(1, [e], [0, 1])[0], e, 2)
+        square("v", 1, slice(0, 2), slice(6, 8))
+        store(1, 0)
+        store(1, 1)
+        for g, t in ((1, 2), (0, 3), (1, 3)):
+            later[g, t] = multiply(1, (low, high)[g], [t])
+        rectify_bank(1, *later[0, 2])
+        add_bias_experts(1, later[1, 2][0], 1, 2)
+        square("v", 1, slice(2, 3), slice(0, E))
+        store(1, 2)
+        rectify_bank(1, *later[0, 3])
+        rectify_bank(1, *later[1, 3])
+        square("v", 1, slice(3, 4), slice(0, G))
+        square("s", 1, slice(3, 4), slice(G, E))
+        store(1, 3)

@@ -185,7 +185,7 @@ def tile_moe_eps_lin_relu2_kernel(tc, xT, w_words, w_scales, b, offs, out):
         for e in range(E):
             for a in range(2):
                 gather_words(1, [e], a)
-        for g, engines in enumerate(("gggg", "ggss")):
+        for g, engines in enumerate(("gggg", "ssgg")):
             for t in range(4):
                 rectify_bank(0, *multiply(0, (low, high)[g], [t]))
                 square(engines[t], 0, slice(t, t + 1), slice(G * g, G * (g + 1)))
@@ -194,7 +194,7 @@ def tile_moe_eps_lin_relu2_kernel(tc, xT, w_words, w_scales, b, offs, out):
         later = {}
         for pair in range(3):
             rectify_bank(1, *multiply(1, [2 * pair, 2 * pair + 1], [0, 1]))
-            square("ggs"[pair], 1, slice(0, 2), slice(2 * pair, 2 * pair + 2))
+            square("gss"[pair], 1, slice(0, 2), slice(2 * pair, 2 * pair + 2))
             if pair == 1:
                 later[0, 2] = multiply(1, low, [2])
         for e in (6, 7):

@@ -165,9 +165,8 @@ def tile_moe_eps_lin_relu2_kernel(tc, xT, w_words, w_scales, b, offs, out):
         interleave(nc.scalar.copy, 0, 0, 352, 512)
         load_weight_words(0, "raw00")
         quantize(0, 0)
-        interleave(nc.vector.tensor_copy, 0, 1, 0, 64)
         gather_words(0, range(E), 0)
-        interleave(nc.scalar.copy, 0, 1, 64, 512)
+        interleave(nc.scalar.copy, 0, 1, 0, 512)
         quantize(0, 1)
         for experts in (low, high):
             gather_scales(0, experts)

@@ -6,7 +6,6 @@ K, T, E, C, N, R = 1024, 1024, 8, 256, 512, 8
 U = C // R
 P = 128
 HALF = T // 2
-G = 4
 FLOPS = 2 * E * C * K * N
 
 F32 = mybir.dt.float32
@@ -31,31 +30,44 @@ def tile_moe_eps_lin_relu2_kernel(tc, xT, w_words, w_scales, b, offs, out):
         psum = ctx.enter_context(tc.psum_pool(name="psum", bufs=8))
 
         offsets = keep.tile([P, E * C // 16], U16, name="offsets")
-        raw = [[keep.tile([P, 4, HALF], F32, align_bytes=64, name=f"raw{h}{a}") for a in range(2)] for h in range(2)]
-        grouped = [[keep.tile([P, HALF, 4], BF16, align_bytes=64, name=f"grouped{h}{a}") for a in range(2)] for h in range(2)]
-        words = [keep.tile([P, T], U32, align_bytes=64, name=f"words{a}") for a in range(2)]
-        scales = keep.tile([P, T], U8, align_bytes=64, name="scales")
-        slot_words = {}
-        slot_scales = [[keep.tile([P, E * P], U8, align_bytes=64, name=f"slot_scales{h}")] for h in range(2)]
-        ww = []
-        ws = []
+        raw = [[keep.tile([P, 4, HALF], F32, align_bytes=256, name=f"raw{h}{a}") for a in range(2)] for h in range(2)]
+        grouped = [[keep.tile([P, HALF, 4], BF16, align_bytes=256, name=f"grouped{h}{a}") for a in range(2)] for h in range(2)]
+        words = [keep.tile([P, T], U32, align_bytes=256, name=f"words{a}") for a in range(2)]
+        scales = keep.tile([P, T], U8, align_bytes=256, name="scales")
+        both = [keep.tile([P, E * P], U8, align_bytes=256, name=f"both{h}") for h in range(2)]
         bias = keep.tile([P, N // P, E], F32, name="bias")
         results = [keep.tile([P, 4, R // 2, E, U], F32, name=f"results{h}") for h in range(2)]
+        slot_words = {}
+        second = {}
+        ww = {}
+        ws = {}
 
         def load_x(h, a):
             rows = xT[512 * a : 512 * (a + 1), HALF * h : HALF * (h + 1)]
             nc.sync.dma_start(raw[h][a][:], rows.rearrange("(p j) w -> p j w", j=4))
 
-        def load_weight_scales(tag):
-            ws.append(keep.tile([P, 2 * E, N], U8, align_bytes=64, name="ws", tag=tag))
-            rows = w_scales.bitcast(I32).rearrange("e a (q r) n -> r q (e a) n", r=4)
+        def load_weight_scales(queue, experts, tag):
+            lo, n = experts[0], len(experts)
+            tile = keep.tile([P, 2 * n, N], U8, align_bytes=256, name=f"ws{lo}", tag=tag)
+            rows = w_scales[lo : lo + n].bitcast(I32).rearrange("e a (q r) n -> r q (e a) n", r=4)
             for r in range(4):
-                nc.gpsimd.dma_start(ws[0][r:P:32, :, :].bitcast(I32), rows[r])
+                queue.dma_start(tile[r:P:32, :, :].bitcast(I32), rows[r])
+            for e in experts:
+                ws[e] = tile[:, 2 * (e - lo) : 2 * (e - lo + 1), :]
 
-        def load_weight_words(g, tag):
-            ww.append(keep.tile([P, 2 * G, 2 * N], U8, align_bytes=64, name=f"ww{g}", tag=tag))
-            rows = w_words[G * g : G * (g + 1)].bitcast(I32).rearrange("e a p n -> p (e a) n")
-            nc.sync.dma_start(ww[g][:].bitcast(I32), rows)
+        def load_weight_words(groups, tag=None):
+            first, last = groups[0][0], groups[-1][-1]
+            tile = keep.tile([P, (last + 1 - first) * 4 * N], U8, align_bytes=256, name=f"ww{first}", tag=tag or f"ww{first}")
+            for experts in groups:
+                lo, n = experts[0], len(experts)
+                part = tile[:, (lo - first) * 4 * N : (lo - first + n) * 4 * N]
+                rows = w_words[lo : lo + n].bitcast(I32).rearrange("e a p n -> p (e a) n")
+                nc.sync.dma_start(part.bitcast(I32).rearrange("p (x n) -> p x n", x=2 * n), rows)
+                for e in experts:
+                    ww[e] = tile[:, (e - first) * 4 * N : (e - first + 1) * 4 * N]
+
+        def load_bias(queue):
+            queue.dma_start(bias[:], b.rearrange("(t p) e -> p t e", p=P))
 
         def interleave(copy, h, a, lo, hi):
             copy(
@@ -76,45 +88,73 @@ def tile_moe_eps_lin_relu2_kernel(tc, xT, w_words, w_scales, b, offs, out):
             window = table[:, : HALF * (h + 1)]
             nc.vector.tensor_copy(target, window.indirect(offsets[:, first : first + P // 16]))
 
-        def gather_words(h, experts, a, tag=None):
+        def word_tile(h, experts, a, tag=None):
             name = f"slot_words{h}{experts[0]}{a}"
-            tile = keep.tile([P, len(experts) * P], U32, align_bytes=64, name=name, tag=tag or name)
+            tile = keep.tile([P, len(experts) * P], U32, align_bytes=256, name=name, tag=tag or name)
             for i, e in enumerate(experts):
                 slot_words[h, e, a] = tile[:, P * i : P * (i + 1)]
-                gather(slot_words[h, e, a], words[a], h, e)
+
+        def gather_words(h, experts, passes):
+            for e in experts:
+                for a in passes:
+                    gather(slot_words[h, e, a], words[a], h, e)
 
         def gather_scales(h, experts):
             for e in experts:
-                gather(slot_scales[h][0][:, P * e : P * (e + 1)], scales, h, e)
+                gather(both[h][:, P * e : P * (e + 1)], scales, h, e)
 
-        def second_plane(h, tag):
-            plane = keep.tile([P, E * P], U8, align_bytes=64, name=f"second{h}", tag=tag)
-            slot_scales[h].append(plane)
-
-        def move_scales(h, queue, experts):
-            both, second = slot_scales[h]
-            cols = slice(P * experts[0], P * (experts[-1] + 1))
-            for lo, count in ((0, 64), (64, 32), (96, 4)):
-                queue.dma_start(second[lo : lo + count, cols].bitcast(I32), both[lo + 4 : lo + 4 + count, cols].bitcast(I32))
+        def move_scales(h, queue, experts, tag=None):
+            lo, n = experts[0], len(experts)
+            name = f"second{h}{lo}"
+            tile = keep.tile([P, n * P], U8, align_bytes=256, name=name, tag=tag or name)
+            for r in range(4):
+                queue.dma_start(tile[r:P:32, :].bitcast(I32), both[h][r + 4 : P : 32, P * lo : P * (lo + n)].bitcast(I32))
+            for e in experts:
+                second[h, e] = tile[:, P * (e - lo) : P * (e - lo + 1)]
 
         def product(target, h, e, t):
-            g, i = divmod(e, G)
-            for a in range(2):
+            for a in (1, 0):
                 nc.tensor.matmul_mx(
                     out=target,
-                    lhsT=ww[g][:, 2 * i + a, 2 * P * t : 2 * P * (t + 1)].bitcast(FP4X4),
-                    lhsT_scale=ws[0][:, 2 * e + a, P * t : P * (t + 1)],
+                    lhsT=ww[e][:, 2 * (N * a + P * t) : 2 * (N * a + P * (t + 1))].bitcast(FP4X4),
+                    lhsT_scale=ws[e][:, a, P * t : P * (t + 1)],
                     rhs=slot_words[h, e, a].bitcast(FP8X4),
-                    rhs_scale=slot_scales[h][a][:, P * e : P * (e + 1)],
-                    start=(a == 0),
-                    stop=(a == 1),
+                    rhs_scale=second[h, e] if a == 1 else both[h][:, P * e : P * (e + 1)],
+                    start=(a == 1),
+                    stop=(a == 0),
                 )
 
-        def rectify(sums, h, e, t):
-            nc.scalar.activation(results[h][:, t, :, e, :], sums.rearrange("p (m u) -> p m u", u=U), RELU, bias=bias[:, t, e : e + 1])
+        def multiply(h, experts, tiles):
+            bank = psum.tile([P, len(experts), len(tiles), P], F32, name="bank")
+            for i, e in enumerate(experts):
+                for j, t in enumerate(tiles):
+                    product(bank[:, i, j, :], h, e, t)
+            return bank, h, experts, tiles
 
-        def square(engine, h, tiles, experts):
-            v = results[h][:, tiles, :, experts, :].rearrange("p t m e u -> p (t m) (e u)")
+        def rectify(job):
+            bank, h, experts, tiles = job
+            for j, t in enumerate(tiles):
+                for i, e in enumerate(experts):
+                    sums = bank[:, i, j, :].rearrange("p (m u) -> p m u", u=U)
+                    nc.scalar.activation(results[h][:, t, :, e, :], sums, RELU, bias=bias[:, t, e : e + 1])
+
+        def add_bias(job):
+            bank, h, experts, tiles = job
+            if len(tiles) == 1:
+                t, es = tiles[0], slice(experts[0], experts[-1] + 1)
+                target = results[h][:, t, :, es, :].rearrange("p m e u -> p e m u")
+                sums = bank[:, :, 0, :].rearrange("p e (m u) -> p e m u", u=U)
+                spread = bias[:, t, es].unsqueeze(2).unsqueeze(3).to_broadcast([P, len(experts), R // 2, U])
+                nc.vector.tensor_tensor(target, sums, spread, ADD)
+            else:
+                ts = slice(tiles[0], tiles[-1] + 1)
+                for i, e in enumerate(experts):
+                    sums = bank[:, i, :, :].rearrange("p t (m u) -> p t m u", u=U)
+                    spread = bias[:, ts, e].unsqueeze(2).unsqueeze(3).to_broadcast([P, len(tiles), R // 2, U])
+                    nc.vector.tensor_tensor(results[h][:, ts, :, e, :], sums, spread, ADD)
+
+        def square(engine, h, experts, tiles):
+            v = results[h][:, tiles[0] : tiles[-1] + 1, :, experts[0] : experts[-1] + 1, :].rearrange("p t m e u -> p (t m) (e u)")
             if engine == "s":
                 nc.scalar.activation(v, v, SQUARE)
             elif engine == "v":
@@ -122,93 +162,77 @@ def tile_moe_eps_lin_relu2_kernel(tc, xT, w_words, w_scales, b, offs, out):
             else:
                 nc.gpsimd.tensor_tensor(v, v, v, MULT)
 
+        def finish(job, engine):
+            rectify(job)
+            square(engine, job[1], job[2], job[3])
+
+        def finish_on_vector(job):
+            add_bias(job)
+            square("v", job[1], job[2], job[3])
+
         def store(h, t):
             rows = out[P * t : P * (t + 1), T * h : T * (h + 1)]
             nc.sync.dma_start(rows, results[h][:, t].rearrange("p m e u -> p (m e u)"))
 
-        def multiply(h, experts, tiles):
-            bank = psum.tile([P, 4, P], F32, name="bank")
-            pairs = [(e, t) for e in experts for t in tiles]
-            for i, (e, t) in enumerate(pairs):
-                product(bank[:, i, :], h, e, t)
-            return bank, pairs
-
-        def rectify_bank(h, bank, pairs):
-            for i, (e, t) in enumerate(pairs):
-                rectify(bank[:, i, :], h, e, t)
-
-        def add_bias_tiles(h, bank, e, count):
-            sums = bank[:, :count, :].rearrange("p t (m u) -> p t m u", u=U)
-            spread = bias[:, :count, e].unsqueeze(2).unsqueeze(3).to_broadcast([P, count, R // 2, U])
-            nc.vector.tensor_tensor(results[h][:, :count, :, e, :], sums, spread, ADD)
-
-        def add_bias_experts(h, bank, g, t):
-            target = results[h][:, t, :, G * g : G * (g + 1), :].rearrange("p m e u -> p e m u")
-            sums = bank[:].rearrange("p e (m u) -> p e m u", u=U)
-            spread = bias[:, t, G * g : G * (g + 1)].unsqueeze(2).unsqueeze(3).to_broadcast([P, G, R // 2, U])
-            nc.vector.tensor_tensor(target, sums, spread, ADD)
-
-        low, high = range(G), range(G, E)
+        every = range(E)
         nc.gpsimd.memset(scales[:].bitcast(I32), 0)
-        second_plane(0, "second0")
-        second_plane(1, "second1")
 
-        load_weight_scales("ws")
-        nc.scalar.dma_start(bias[:], b.rearrange("(t p) e -> p t e", p=P))
+        load_weight_scales(nc.gpsimd, every, "ws")
+        load_bias(nc.gpsimd)
         load_x(0, 0)
         nc.sync.dma_start(offsets[:], offs)
         load_x(0, 1)
         load_x(1, 0)
+        load_weight_words([[0, 1]])
         load_x(1, 1)
 
         interleave(nc.vector.tensor_copy, 0, 0, 0, 352)
         interleave(nc.scalar.copy, 0, 0, 352, 512)
-        load_weight_words(0, "raw00")
         quantize(0, 0)
-        gather_words(0, range(E), 0)
+        word_tile(0, every, 0)
+        gather_words(0, every, [0])
         interleave(nc.scalar.copy, 0, 1, 0, 512)
         quantize(0, 1)
-        for experts in (low, high):
-            gather_scales(0, experts)
-            move_scales(0, nc.sync, experts)
+        gather_scales(0, every)
+        word_tile(0, every, 1)
+        gather_words(0, every, [1])
         interleave(nc.scalar.copy, 1, 0, 0, 512)
-        load_weight_words(1, "raw10")
+        move_scales(0, nc.sync, every)
+        load_weight_words([[2, 3], [4, 5], [6, 7]], "raw10")
         interleave(nc.scalar.copy, 1, 1, 0, 512)
-        gather_words(0, low, 1)
-        gather_words(0, high, 1)
-        quantize(1, 1)
         quantize(1, 0)
-        for experts in (low, high):
-            gather_scales(1, experts)
-            move_scales(1, nc.sync, experts)
-        for e in range(E):
-            for a in range(2):
-                gather_words(1, [e], a)
-        for g, engines in enumerate(("gggg", "ssgg")):
-            for t in range(4):
-                rectify_bank(0, *multiply(0, (low, high)[g], [t]))
-                square(engines[t], 0, slice(t, t + 1), slice(G * g, G * (g + 1)))
-                if g == 1:
-                    store(0, t)
-        later = {}
-        for pair in range(3):
-            rectify_bank(1, *multiply(1, [2 * pair, 2 * pair + 1], [0, 1]))
-            square("gss"[pair], 1, slice(0, 2), slice(2 * pair, 2 * pair + 2))
-            if pair == 1:
-                later[0, 2] = multiply(1, low, [2])
-        for e in (6, 7):
-            add_bias_tiles(1, multiply(1, [e], [0, 1])[0], e, 2)
-        square("v", 1, slice(0, 2), slice(6, 8))
-        store(1, 0)
-        store(1, 1)
-        for g, t in ((1, 2), (0, 3), (1, 3)):
-            later[g, t] = multiply(1, (low, high)[g], [t])
-        rectify_bank(1, *later[0, 2])
-        add_bias_experts(1, later[1, 2][0], 1, 2)
-        square("v", 1, slice(2, 3), slice(0, E))
+        quantize(1, 1)
+        for group in (range(4), range(4, E)):
+            gather_scales(1, group)
+            move_scales(1, nc.sync, group)
+        word_tile(1, every, 0, "grouped11")
+        word_tile(1, every, 1)
+        gather_words(1, every, [1, 0])
+
+        finish(multiply(0, [0, 1], [0, 1]), "g")
+        finish(multiply(0, [2, 3], [0, 1]), "g")
+        finish(multiply(0, [0, 1], [2, 3]), "g")
+        finish(multiply(0, [4, 5], [0, 1]), "s")
+        for t in (0, 1):
+            finish(multiply(0, [6, 7], [t]), "s")
+            store(0, t)
+        finish(multiply(0, [2, 3], [2, 3]), "g")
+        finish(multiply(0, [4, 5], [2, 3]), "g")
+        finish(multiply(0, [6, 7], [2, 3]), "s")
+        store(0, 2)
+        store(0, 3)
+
+        finish(multiply(1, [0, 1], [0, 1]), "g")
+        finish(multiply(1, [2, 3], [0, 1]), "s")
+        late = [multiply(1, [0, 1], [2, 3])]
+        finish(multiply(1, [4, 5], [0, 1]), "s")
+        late.append(multiply(1, [2, 3], [2, 3]))
+        for t in (0, 1):
+            finish_on_vector(multiply(1, [6, 7], [t]))
+            store(1, t)
+        finish(late[0], "s")
+        finish(late[1], "v")
+        finish(multiply(1, [4, 5], [2, 3]), "s")
+        finish_on_vector(multiply(1, [6, 7], [2, 3]))
         store(1, 2)
-        rectify_bank(1, *later[0, 3])
-        rectify_bank(1, *later[1, 3])
-        square("v", 1, slice(3, 4), slice(0, G))
-        square("s", 1, slice(3, 4), slice(G, E))
         store(1, 3)

@@ -35,7 +35,7 @@ def tile_moe_eps_lin_relu2_kernel(tc, xT, w_words, w_scales, b, offs, out):
         words = [keep.tile([P, T], U32, align_bytes=256, name=f"words{a}") for a in range(2)]
         scales = keep.tile([P, T], U8, align_bytes=256, name="scales")
         both = [keep.tile([P, E * P], U8, align_bytes=256, name=f"both{h}") for h in range(2)]
-        bias = keep.tile([P, N // P, E], F32, name="bias")
+        held = {}
         results = [keep.tile([P, 4, R // 2, E, U], F32, name=f"results{h}") for h in range(2)]
         slot_words = {}
         second = {}
@@ -66,8 +66,9 @@ def tile_moe_eps_lin_relu2_kernel(tc, xT, w_words, w_scales, b, offs, out):
                 for e in experts:
                     ww[e] = tile[:, (e - first) * 4 * N : (e - first + 1) * 4 * N]
 
-        def load_bias(queue):
-            queue.dma_start(bias[:], b.rearrange("(t p) e -> p t e", p=P))
+        def load_bias(queue, tag):
+            held["bias"] = keep.tile([P, N // P, E], F32, align_bytes=256, name="bias", tag=tag)
+            queue.dma_start(held["bias"][:], b.rearrange("(t p) e -> p t e", p=P))
 
         def interleave(copy, h, a, lo, hi):
             copy(
@@ -136,7 +137,7 @@ def tile_moe_eps_lin_relu2_kernel(tc, xT, w_words, w_scales, b, offs, out):
             for j, t in enumerate(tiles):
                 for i, e in enumerate(experts):
                     sums = bank[:, i, j, :].rearrange("p (m u) -> p m u", u=U)
-                    nc.scalar.activation(results[h][:, t, :, e, :], sums, RELU, bias=bias[:, t, e : e + 1])
+                    nc.scalar.activation(results[h][:, t, :, e, :], sums, RELU, bias=held["bias"][:, t, e : e + 1])
 
         def add_bias(job):
             bank, h, experts, tiles = job
@@ -144,13 +145,13 @@ def tile_moe_eps_lin_relu2_kernel(tc, xT, w_words, w_scales, b, offs, out):
                 t, es = tiles[0], slice(experts[0], experts[-1] + 1)
                 target = results[h][:, t, :, es, :].rearrange("p m e u -> p e m u")
                 sums = bank[:, :, 0, :].rearrange("p e (m u) -> p e m u", u=U)
-                spread = bias[:, t, es].unsqueeze(2).unsqueeze(3).to_broadcast([P, len(experts), R // 2, U])
+                spread = held["bias"][:, t, es].unsqueeze(2).unsqueeze(3).to_broadcast([P, len(experts), R // 2, U])
                 nc.vector.tensor_tensor(target, sums, spread, ADD)
             else:
                 ts = slice(tiles[0], tiles[-1] + 1)
                 for i, e in enumerate(experts):
                     sums = bank[:, i, :, :].rearrange("p t (m u) -> p t m u", u=U)
-                    spread = bias[:, ts, e].unsqueeze(2).unsqueeze(3).to_broadcast([P, len(tiles), R // 2, U])
+                    spread = held["bias"][:, ts, e].unsqueeze(2).unsqueeze(3).to_broadcast([P, len(tiles), R // 2, U])
                     nc.vector.tensor_tensor(results[h][:, ts, :, e, :], sums, spread, ADD)
 
         def square(engine, h, experts, tiles):
@@ -177,8 +178,6 @@ def tile_moe_eps_lin_relu2_kernel(tc, xT, w_words, w_scales, b, offs, out):
         every = range(E)
         nc.gpsimd.memset(scales[:].bitcast(I32), 0)
 
-        load_weight_scales(nc.gpsimd, every, "ws")
-        load_bias(nc.gpsimd)
         load_x(0, 0)
         nc.sync.dma_start(offsets[:], offs)
         load_x(0, 1)
@@ -188,7 +187,9 @@ def tile_moe_eps_lin_relu2_kernel(tc, xT, w_words, w_scales, b, offs, out):
 
         interleave(nc.vector.tensor_copy, 0, 0, 0, 352)
         interleave(nc.scalar.copy, 0, 0, 352, 512)
+        load_weight_scales(nc.gpsimd, every, "raw00")
         quantize(0, 0)
+        load_bias(nc.gpsimd, "grouped00")
         word_tile(0, every, 0)
         gather_words(0, every, [0])
         interleave(nc.scalar.copy, 0, 1, 0, 512)

@@ -46,25 +46,23 @@ def tile_moe_eps_lin_relu2_kernel(tc, xT, w_words, w_scales, b, offs, out):
             rows = xT[512 * a : 512 * (a + 1), HALF * h : HALF * (h + 1)]
             nc.sync.dma_start(raw[h][a][:], rows.rearrange("(p j) w -> p j w", j=4))
 
-        def load_weight_scales(queue, experts, tag):
+        def load_weight_scales(queue, tile, experts):
             lo, n = experts[0], len(experts)
-            tile = keep.tile([P, 2 * n, N], U8, align_bytes=256, name=f"ws{lo}", tag=tag)
             rows = w_scales[lo : lo + n].bitcast(I32).rearrange("e a (q r) n -> r q (e a) n", r=4)
             for r in range(4):
-                queue.dma_start(tile[r:P:32, :, :].bitcast(I32), rows[r])
+                queue.dma_start(tile[r:P:32, :].bitcast(I32).rearrange("q (x n) -> q x n", x=2 * n), rows[r])
             for e in experts:
-                ws[e] = tile[:, 2 * (e - lo) : 2 * (e - lo + 1), :]
+                ws[e] = tile[:, (e - lo) * 2 * N : (e - lo + 1) * 2 * N]
 
-        def load_weight_words(groups, tag=None):
-            first, last = groups[0][0], groups[-1][-1]
-            tile = keep.tile([P, (last + 1 - first) * 4 * N], U8, align_bytes=256, name=f"ww{first}", tag=tag or f"ww{first}")
-            for experts in groups:
-                lo, n = experts[0], len(experts)
-                part = tile[:, (lo - first) * 4 * N : (lo - first + n) * 4 * N]
-                rows = w_words[lo : lo + n].bitcast(I32).rearrange("e a p n -> p (e a) n")
-                nc.sync.dma_start(part.bitcast(I32).rearrange("p (x n) -> p x n", x=2 * n), rows)
-                for e in experts:
-                    ww[e] = tile[:, (e - first) * 4 * N : (e - first + 1) * 4 * N]
+        def load_weight_words(tile, experts):
+            lo, n = experts[0], len(experts)
+            rows = w_words[lo : lo + n].bitcast(I32).rearrange("e a p n -> p (e a) n")
+            nc.sync.dma_start(tile.bitcast(I32).rearrange("p (x n) -> p x n", x=2 * n), rows)
+            for e in experts:
+                ww[e] = tile[:, (e - lo) * 4 * N : (e - lo + 1) * 4 * N]
+
+        def byte_tile(name, width, tag=None):
+            return keep.tile([P, width], U8, align_bytes=256, name=name, tag=tag or name)
 
         def load_bias(queue, tag):
             held["bias"] = keep.tile([P, N // P, E], F32, align_bytes=256, name="bias", tag=tag)
@@ -118,7 +116,7 @@ def tile_moe_eps_lin_relu2_kernel(tc, xT, w_words, w_scales, b, offs, out):
                 nc.tensor.matmul_mx(
                     out=target,
                     lhsT=ww[e][:, 2 * (N * a + P * t) : 2 * (N * a + P * (t + 1))].bitcast(FP4X4),
-                    lhsT_scale=ws[e][:, a, P * t : P * (t + 1)],
+                    lhsT_scale=ws[e][:, N * a + P * t : N * a + P * (t + 1)],
                     rhs=slot_words[h, e, a].bitcast(FP8X4),
                     rhs_scale=second[h, e] if a == 1 else both[h][:, P * e : P * (e + 1)],
                     start=(a == 1),
@@ -182,12 +180,12 @@ def tile_moe_eps_lin_relu2_kernel(tc, xT, w_words, w_scales, b, offs, out):
         nc.sync.dma_start(offsets[:], offs)
         load_x(0, 1)
         load_x(1, 0)
-        load_weight_words([[0, 1]])
         load_x(1, 1)
+        load_weight_words(byte_tile("first_weights", 8 * N)[:], [0, 1])
 
         interleave(nc.vector.tensor_copy, 0, 0, 0, 352)
         interleave(nc.scalar.copy, 0, 0, 352, 512)
-        load_weight_scales(nc.gpsimd, every, "raw00")
+        load_weight_scales(nc.gpsimd, byte_tile("weight_scales", 16 * N, "raw00")[:], every)
         quantize(0, 0)
         load_bias(nc.gpsimd, "grouped00")
         word_tile(0, every, 0)
@@ -199,16 +197,22 @@ def tile_moe_eps_lin_relu2_kernel(tc, xT, w_words, w_scales, b, offs, out):
         gather_words(0, every, [1])
         interleave(nc.scalar.copy, 1, 0, 0, 512)
         move_scales(0, nc.sync, every)
-        load_weight_words([[2, 3], [4, 5], [6, 7]], "raw10")
+        later = byte_tile("later_weights", 24 * N, "raw10")
+        load_weight_words(later[:, : 8 * N], [2, 3])
+        load_weight_words(later[:, 8 * N : 16 * N], [4, 5])
+        load_weight_words(later[:, 16 * N : 24 * N], [6, 7])
         interleave(nc.scalar.copy, 1, 1, 0, 512)
         quantize(1, 0)
+        word_tile(1, [0, 1], 0)
+        gather_words(1, [0, 1], [0])
         quantize(1, 1)
         for group in (range(4), range(4, E)):
             gather_scales(1, group)
             move_scales(1, nc.sync, group)
-        word_tile(1, every, 0, "grouped11")
+        word_tile(1, range(2, E), 0, "grouped11")
         word_tile(1, every, 1)
-        gather_words(1, every, [1, 0])
+        gather_words(1, [0, 1], [1])
+        gather_words(1, range(2, E), [1, 0])
 
         finish(multiply(0, [0, 1], [0, 1]), "g")
         finish(multiply(0, [2, 3], [0, 1]), "g")

@@ -111,24 +111,35 @@ def tile_moe_eps_lin_relu2_kernel(tc, xT, w_words, w_scales, b, offs, out):
             for e in experts:
                 second[h, e] = tile[:, P * (e - lo) : P * (e - lo + 1)]
 
-        def product(target, h, e, t):
-            for a in (1, 0):
-                nc.tensor.matmul_mx(
-                    out=target,
-                    lhsT=ww[e][:, 2 * (N * a + P * t) : 2 * (N * a + P * (t + 1))].bitcast(FP4X4),
-                    lhsT_scale=ws[e][:, N * a + P * t : N * a + P * (t + 1)],
-                    rhs=slot_words[h, e, a].bitcast(FP8X4),
-                    rhs_scale=second[h, e] if a == 1 else both[h][:, P * e : P * (e + 1)],
-                    start=(a == 1),
-                    stop=(a == 0),
-                )
+        def product(target, h, e, t, a, start, stop):
+            nc.tensor.matmul_mx(
+                out=target,
+                lhsT=ww[e][:, 2 * (N * a + P * t) : 2 * (N * a + P * (t + 1))].bitcast(FP4X4),
+                lhsT_scale=ws[e][:, N * a + P * t : N * a + P * (t + 1)],
+                rhs=slot_words[h, e, a].bitcast(FP8X4),
+                rhs_scale=second[h, e] if a == 1 else both[h][:, P * e : P * (e + 1)],
+                start=start,
+                stop=stop,
+            )
 
         def multiply(h, experts, tiles):
             bank = psum.tile([P, len(experts), len(tiles), P], F32, name="bank")
             for i, e in enumerate(experts):
                 for j, t in enumerate(tiles):
-                    product(bank[:, i, j, :], h, e, t)
+                    product(bank[:, i, j, :], h, e, t, 1, True, False)
+                    product(bank[:, i, j, :], h, e, t, 0, False, True)
             return bank, h, experts, tiles
+
+        def multiply_by_passes(h, experts, tile_sets):
+            banks = [psum.tile([P, len(experts), len(tiles), P], F32, name="bank") for tiles in tile_sets]
+            for a in range(2):
+                for bank, tiles in zip(banks, tile_sets):
+                    for i, e in enumerate(experts):
+                        for j, t in enumerate(tiles):
+                            first = a == 0 and i == 0 and j == 0
+                            last = a == 1 and i == len(experts) - 1 and j == len(tiles) - 1
+                            product(bank[:, i, j, :], h, e, t, a, first, last)
+            return [(bank, h, experts, tiles) for bank, tiles in zip(banks, tile_sets)]
 
         def rectify(job):
             bank, h, experts, tiles = job
@@ -181,13 +192,13 @@ def tile_moe_eps_lin_relu2_kernel(tc, xT, w_words, w_scales, b, offs, out):
         load_x(0, 1)
         load_x(1, 0)
         load_x(1, 1)
-        load_weight_words(byte_tile("first_weights", 8 * N)[:], [0, 1])
+        load_weight_words(byte_tile("first_weights", 4 * N)[:], [0])
 
         interleave(nc.vector.tensor_copy, 0, 0, 0, 352)
         interleave(nc.scalar.copy, 0, 0, 352, 512)
-        load_weight_scales(nc.gpsimd, byte_tile("weight_scales", 16 * N, "raw00")[:], every)
+        load_bias(nc.gpsimd, "raw00")
         quantize(0, 0)
-        load_bias(nc.gpsimd, "grouped00")
+        load_weight_scales(nc.gpsimd, byte_tile("weight_scales", 16 * N, "grouped00")[:], every)
         word_tile(0, every, 0)
         gather_words(0, every, [0])
         interleave(nc.scalar.copy, 0, 1, 0, 512)
@@ -197,12 +208,12 @@ def tile_moe_eps_lin_relu2_kernel(tc, xT, w_words, w_scales, b, offs, out):
         gather_words(0, every, [1])
         interleave(nc.scalar.copy, 1, 0, 0, 512)
         move_scales(0, nc.sync, every)
-        later = byte_tile("later_weights", 24 * N, "raw10")
-        load_weight_words(later[:, : 8 * N], [2, 3])
-        load_weight_words(later[:, 8 * N : 16 * N], [4, 5])
-        load_weight_words(later[:, 16 * N : 24 * N], [6, 7])
-        interleave(nc.scalar.copy, 1, 1, 0, 512)
+        later = byte_tile("later_weights", 28 * N, "raw10")
+        for experts in ([1], [2, 3], [4, 5], [6, 7]):
+            load_weight_words(later[:, 4 * N * (experts[0] - 1) : 4 * N * experts[-1]], experts)
+        interleave(nc.scalar.copy, 1, 1, 192, 512)
         quantize(1, 0)
+        interleave(nc.vector.tensor_copy, 1, 1, 0, 192)
         word_tile(1, [0, 1], 0)
         gather_words(1, [0, 1], [0])
         quantize(1, 1)
@@ -214,30 +225,32 @@ def tile_moe_eps_lin_relu2_kernel(tc, xT, w_words, w_scales, b, offs, out):
         gather_words(1, [0, 1], [1])
         gather_words(1, range(2, E), [1, 0])
 
-        finish(multiply(0, [0, 1], [0, 1]), "g")
+        finish(multiply(0, [0], range(4)), "g")
+        finish(multiply(0, [1], range(4)), "g")
         finish(multiply(0, [2, 3], [0, 1]), "g")
-        finish(multiply(0, [0, 1], [2, 3]), "g")
+        finish(multiply(0, [2, 3], [2, 3]), "g")
         finish(multiply(0, [4, 5], [0, 1]), "s")
         for t in (0, 1):
             finish(multiply(0, [6, 7], [t]), "s")
             store(0, t)
-        finish(multiply(0, [2, 3], [2, 3]), "g")
         finish(multiply(0, [4, 5], [2, 3]), "g")
         finish(multiply(0, [6, 7], [2, 3]), "s")
         store(0, 2)
         store(0, 3)
 
         finish(multiply(1, [0, 1], [0, 1]), "g")
-        finish(multiply(1, [2, 3], [0, 1]), "s")
+        finish(multiply(1, [2, 3], [0, 1]), "g")
         late = [multiply(1, [0, 1], [2, 3])]
         finish(multiply(1, [4, 5], [0, 1]), "s")
-        late.append(multiply(1, [2, 3], [2, 3]))
         for t in (0, 1):
             finish_on_vector(multiply(1, [6, 7], [t]))
             store(1, t)
-        finish(late[0], "s")
-        finish(late[1], "v")
-        finish(multiply(1, [4, 5], [2, 3]), "s")
-        finish_on_vector(multiply(1, [6, 7], [2, 3]))
+        late.append(multiply(1, [2, 3], [2, 3]))
+        rectify(late[0])
+        rectify(late[1])
+        add_bias(multiply(1, range(4, E), [2]))
+        square("v", 1, every, [2])
         store(1, 2)
+        finish(multiply(1, range(4, E), [3]), "s")
+        square("v", 1, range(4), [3])
         store(1, 3)

@@ -211,12 +211,13 @@ def tile_moe_eps_lin_relu2_kernel(tc, xT, w_words, w_scales, b, offs, out):
         later = byte_tile("later_weights", 28 * N, "raw10")
         for experts in ([1], [2, 3], [4, 5], [6, 7]):
             load_weight_words(later[:, 4 * N * (experts[0] - 1) : 4 * N * experts[-1]], experts)
-        interleave(nc.scalar.copy, 1, 1, 192, 512)
+        interleave(nc.scalar.copy, 1, 1, 0, 512)
         quantize(1, 0)
-        interleave(nc.vector.tensor_copy, 1, 1, 0, 192)
-        word_tile(1, [0, 1], 0)
-        gather_words(1, [0, 1], [0])
+        word_tile(1, [0], 0)
+        gather_words(1, [0], [0])
         quantize(1, 1)
+        word_tile(1, [1], 0, "raw11")
+        gather_words(1, [1], [0])
         for group in (range(4), range(4, E)):
             gather_scales(1, group)
             move_scales(1, nc.sync, group)
@@ -239,11 +240,13 @@ def tile_moe_eps_lin_relu2_kernel(tc, xT, w_words, w_scales, b, offs, out):
         store(0, 3)
 
         finish(multiply(1, [0, 1], [0, 1]), "g")
-        finish(multiply(1, [2, 3], [0, 1]), "g")
+        finish(multiply(1, [2, 3], [0, 1]), "s")
         late = [multiply(1, [0, 1], [2, 3])]
         finish(multiply(1, [4, 5], [0, 1]), "s")
+        for e in (6, 7):
+            add_bias(multiply(1, [e], [0, 1]))
         for t in (0, 1):
-            finish_on_vector(multiply(1, [6, 7], [t]))
+            square("v", 1, [6, 7], [t])
             store(1, t)
         late.append(multiply(1, [2, 3], [2, 3]))
         rectify(late[0])

@@ -54,12 +54,18 @@ def tile_moe_eps_lin_relu2_kernel(tc, xT, w_words, w_scales, b, offs, out):
             for e in experts:
                 ws[e] = tile[:, (e - lo) * 2 * N : (e - lo + 1) * 2 * N]
 
-        def load_weight_words(tile, experts):
-            lo, n = experts[0], len(experts)
-            rows = w_words[lo : lo + n].bitcast(I32).rearrange("e a p n -> p (e a) n")
-            nc.sync.dma_start(tile.bitcast(I32).rearrange("p (x n) -> p x n", x=2 * n), rows)
+        def load_weight_words(tile, experts, tiles):
+            lo, n, width = experts[0], len(experts), 2 * P * len(tiles)
+            rows = w_words[lo : lo + n, :, :, 2 * P * tiles[0] : 2 * P * (tiles[-1] + 1)]
+            nc.sync.dma_start(
+                tile.bitcast(I32).rearrange("p (x n) -> p x n", x=2 * n),
+                rows.bitcast(I32).rearrange("e a p n -> p (e a) n"),
+            )
             for e in experts:
-                ww[e] = tile[:, (e - lo) * 4 * N : (e - lo + 1) * 4 * N]
+                for a in range(2):
+                    for t in tiles:
+                        first = (2 * (e - lo) + a) * width + 2 * P * (t - tiles[0])
+                        ww[e, a, t] = tile[:, first : first + 2 * P]
 
         def byte_tile(name, width, tag=None):
             return keep.tile([P, width], U8, align_bytes=256, name=name, tag=tag or name)
@@ -114,7 +120,7 @@ def tile_moe_eps_lin_relu2_kernel(tc, xT, w_words, w_scales, b, offs, out):
         def product(target, h, e, t, a, start, stop):
             nc.tensor.matmul_mx(
                 out=target,
-                lhsT=ww[e][:, 2 * (N * a + P * t) : 2 * (N * a + P * (t + 1))].bitcast(FP4X4),
+                lhsT=ww[e, a, t].bitcast(FP4X4),
                 lhsT_scale=ws[e][:, N * a + P * t : N * a + P * (t + 1)],
                 rhs=slot_words[h, e, a].bitcast(FP8X4),
                 rhs_scale=second[h, e] if a == 1 else both[h][:, P * e : P * (e + 1)],
@@ -192,7 +198,7 @@ def tile_moe_eps_lin_relu2_kernel(tc, xT, w_words, w_scales, b, offs, out):
         load_x(0, 1)
         load_x(1, 0)
         load_x(1, 1)
-        load_weight_words(byte_tile("first_weights", 4 * N)[:], [0])
+        load_weight_words(byte_tile("first_weights", 4 * N)[:], [0], range(4))
 
         interleave(nc.vector.tensor_copy, 0, 0, 0, 352)
         interleave(nc.scalar.copy, 0, 0, 352, 512)
@@ -209,8 +215,10 @@ def tile_moe_eps_lin_relu2_kernel(tc, xT, w_words, w_scales, b, offs, out):
         interleave(nc.scalar.copy, 1, 0, 0, 512)
         move_scales(0, nc.sync, every)
         later = byte_tile("later_weights", 28 * N, "raw10")
-        for experts in ([1], [2, 3], [4, 5], [6, 7]):
-            load_weight_words(later[:, 4 * N * (experts[0] - 1) : 4 * N * experts[-1]], experts)
+        load_weight_words(later[:, : 4 * N], [1], range(4))
+        load_weight_words(later[:, 4 * N : 12 * N], [2, 3], range(4))
+        load_weight_words(later[:, 12 * N : 20 * N], range(4, E), [0, 1])
+        load_weight_words(later[:, 20 * N :], range(4, E), [2, 3])
         interleave(nc.scalar.copy, 1, 1, 0, 512)
         quantize(1, 0)
         word_tile(1, [0], 0)
@@ -230,14 +238,9 @@ def tile_moe_eps_lin_relu2_kernel(tc, xT, w_words, w_scales, b, offs, out):
         finish(multiply(0, [1], range(4)), "g")
         finish(multiply(0, [2, 3], [0, 1]), "g")
         finish(multiply(0, [2, 3], [2, 3]), "g")
-        finish(multiply(0, [4, 5], [0, 1]), "s")
-        for t in (0, 1):
-            finish(multiply(0, [6, 7], [t]), "s")
+        for t, engine in enumerate("ssgs"):
+            finish(multiply(0, range(4, E), [t]), engine)
             store(0, t)
-        finish(multiply(0, [4, 5], [2, 3]), "g")
-        finish(multiply(0, [6, 7], [2, 3]), "s")
-        store(0, 2)
-        store(0, 3)
 
         finish(multiply(1, [0, 1], [0, 1]), "g")
         finish(multiply(1, [2, 3], [0, 1]), "s")

@@ -178,13 +178,27 @@ def tile_moe_eps_lin_relu2_kernel(tc, xT, w_words, w_scales, b, offs, out):
             else:
                 nc.gpsimd.tensor_tensor(v, v, v, MULT)
 
+        def vector_pass(job, t, second_step):
+            bank, h, experts, tiles = job
+            sums = bank[:, 0, tiles.index(t), :].rearrange("p (m u) -> p m u", u=U)
+            target = results[h][:, t, :, experts[0], :]
+            column = held["bias"][:, t, experts[0] : experts[0] + 1]
+            if second_step:
+                nc.vector.scalar_tensor_tensor(target, sums, column, target, ADD, MULT)
+            else:
+                nc.vector.tensor_scalar(target, sums, column, 0.0, ADD, MAX)
+
         def finish(job, engine):
             rectify(job)
             square(engine, job[1], job[2], job[3])
 
         def finish_on_vector(job):
-            add_bias(job)
-            square("v", job[1], job[2], job[3])
+            bank, h, experts, tiles = job
+            pairs = [(bank[:, i : i + 2], h, experts[i : i + 2], tiles) for i in range(0, len(experts), 2)]
+            for pair in pairs:
+                add_bias(pair)
+            for pair in pairs:
+                square("v", h, pair[2], tiles)
 
         def store(h, t):
             rows = out[P * t : P * (t + 1), T * h : T * (h + 1)]
@@ -242,21 +256,19 @@ def tile_moe_eps_lin_relu2_kernel(tc, xT, w_words, w_scales, b, offs, out):
             finish(multiply(0, range(4, E), [t]), engine)
             store(0, t)
 
-        finish(multiply(1, [0, 1], [0, 1]), "g")
-        finish(multiply(1, [2, 3], [0, 1]), "s")
-        late = [multiply(1, [0, 1], [2, 3])]
-        finish(multiply(1, [4, 5], [0, 1]), "s")
+        low, high = range(4), range(4, E)
+        finish(multiply(1, low, [0]), "g")
+        early = [multiply(1, low, [1])]
+        finish(multiply(1, [4, 5], [0]), "s")
+        early.append(multiply(1, low, [2]))
         for e in (6, 7):
-            add_bias(multiply(1, [e], [0, 1]))
-        for t in (0, 1):
-            square("v", 1, [6, 7], [t])
+            add_bias(multiply(1, [e], [0]))
+        square("v", 1, [6, 7], [0])
+        store(1, 0)
+        for t in (1, 2):
+            finish(early[t - 1], "s")
+            finish_on_vector(multiply(1, high, [t]))
             store(1, t)
-        late.append(multiply(1, [2, 3], [2, 3]))
-        rectify(late[0])
-        rectify(late[1])
-        add_bias(multiply(1, range(4, E), [2]))
-        square("v", 1, every, [2])
-        store(1, 2)
-        finish(multiply(1, range(4, E), [3]), "s")
-        square("v", 1, range(4), [3])
+        finish(multiply(1, low, [3]), "s")
+        finish_on_vector(multiply(1, high, [3]))
         store(1, 3)

@@ -42,9 +42,9 @@ def tile_moe_eps_lin_relu2_kernel(tc, xT, w_words, w_scales, b, offs, out):
         ww = {}
         ws = {}
 
-        def load_x(h, a):
-            rows = xT[512 * a : 512 * (a + 1), HALF * h : HALF * (h + 1)]
-            nc.sync.dma_start(raw[h][a][:], rows.rearrange("(p j) w -> p j w", j=4))
+        def load_x(h, a, lo=0, hi=HALF):
+            rows = xT[512 * a : 512 * (a + 1), HALF * h + lo : HALF * h + hi]
+            nc.sync.dma_start(raw[h][a][:, :, lo:hi], rows.rearrange("(p j) w -> p j w", j=4))
 
         def load_weight_scales(queue, tile, experts):
             lo, n = experts[0], len(experts)
@@ -80,12 +80,12 @@ def tile_moe_eps_lin_relu2_kernel(tc, xT, w_words, w_scales, b, offs, out):
                 in_=raw[h][a][:, :, lo:hi].rearrange("p j (g i) -> p g j i", i=4),
             )
 
-        def quantize(h, a):
-            cols = slice(HALF * h, HALF * (h + 1))
+        def quantize(h, a, lo=0, hi=HALF):
+            cols = slice(HALF * h + lo, HALF * h + hi)
             nc.vector.quantize_mx(
                 out=words[a][:, cols].bitcast(FP8X4),
                 scales=scales[4 * a : P, cols],
-                in_=grouped[h][a][:].rearrange("p w j -> p (w j)"),
+                in_=grouped[h][a][:, lo:hi, :].rearrange("p w j -> p (w j)"),
             )
 
         def gather(target, table, h, e):
@@ -207,21 +207,27 @@ def tile_moe_eps_lin_relu2_kernel(tc, xT, w_words, w_scales, b, offs, out):
         every = range(E)
         nc.gpsimd.memset(scales[:].bitcast(I32), 0)
 
-        load_x(0, 0)
+        load_x(0, 0, 0, 256)
+        load_x(0, 0, 256, 512)
         nc.sync.dma_start(offsets[:], offs)
-        load_x(0, 1)
+        load_x(0, 1, 0, 256)
+        load_x(0, 1, 256, 512)
         load_x(1, 0)
         load_x(1, 1)
         load_weight_words(byte_tile("first_weights", 4 * N)[:], [0], range(4))
 
-        interleave(nc.vector.tensor_copy, 0, 0, 0, 352)
-        interleave(nc.scalar.copy, 0, 0, 352, 512)
-        load_bias(nc.gpsimd, "raw00")
-        quantize(0, 0)
-        load_weight_scales(nc.gpsimd, byte_tile("weight_scales", 16 * N, "grouped00")[:], every)
+        interleave(nc.vector.tensor_copy, 0, 0, 0, 176)
+        interleave(nc.scalar.copy, 0, 0, 176, 256)
+        quantize(0, 0, 0, 256)
+        interleave(nc.vector.tensor_copy, 0, 0, 256, 432)
+        interleave(nc.scalar.copy, 0, 0, 432, 512)
+        load_weight_scales(nc.gpsimd, byte_tile("weight_scales", 16 * N, "raw00")[:], every)
+        quantize(0, 0, 256, 512)
+        load_bias(nc.gpsimd, "grouped00")
         word_tile(0, every, 0)
         gather_words(0, every, [0])
-        interleave(nc.scalar.copy, 0, 1, 0, 512)
+        interleave(nc.scalar.copy, 0, 1, 0, 256)
+        interleave(nc.scalar.copy, 0, 1, 256, 512)
         quantize(0, 1)
         gather_scales(0, every)
         word_tile(0, every, 1)
@@ -235,29 +241,31 @@ def tile_moe_eps_lin_relu2_kernel(tc, xT, w_words, w_scales, b, offs, out):
         load_weight_words(later[:, 20 * N :], range(4, E), [2, 3])
         interleave(nc.scalar.copy, 1, 1, 0, 512)
         quantize(1, 0)
-        word_tile(1, [0], 0)
-        gather_words(1, [0], [0])
+        word_tile(1, range(3), 0)
+        gather_words(1, range(3), [0])
         quantize(1, 1)
-        word_tile(1, [1], 0, "raw11")
-        gather_words(1, [1], [0])
+        word_tile(1, [3], 0, "raw11")
+        gather_words(1, [3], [0])
         for group in (range(4), range(4, E)):
             gather_scales(1, group)
             move_scales(1, nc.sync, group)
-        word_tile(1, range(2, E), 0, "grouped11")
+        word_tile(1, range(4, E), 0, "grouped11")
         word_tile(1, every, 1)
-        gather_words(1, [0, 1], [1])
-        gather_words(1, range(2, E), [1, 0])
+        gather_words(1, range(4), [1])
+        gather_words(1, range(4, E), [1, 0])
 
         finish(multiply(0, [0], range(4)), "g")
         finish(multiply(0, [1], range(4)), "g")
         finish(multiply(0, [2, 3], [0, 1]), "g")
         finish(multiply(0, [2, 3], [2, 3]), "g")
-        for t, engine in enumerate("ssgs"):
-            finish(multiply(0, range(4, E), [t]), engine)
-            store(0, t)
-
         low, high = range(4), range(4, E)
+        for t, engine in enumerate("ssg"):
+            finish(multiply(0, high, [t]), engine)
+            store(0, t)
+        waiting = multiply(0, high, [3])
         finish(multiply(1, low, [0]), "g")
+        finish(waiting, "s")
+        store(0, 3)
         early = [multiply(1, low, [1])]
         finish(multiply(1, [4, 5], [0]), "s")
         early.append(multiply(1, low, [2]))

@@ -230,8 +230,8 @@ def tile_moe_eps_lin_relu2_kernel(tc, xT, w_words, w_scales, b, offs, out):
         interleave(nc.scalar.copy, 0, 1, 256, 512)
         quantize(0, 1)
         gather_scales(0, every)
-        word_tile(0, every, 1)
-        gather_words(0, every, [1])
+        word_tile(0, range(5), 1)
+        gather_words(0, range(5), [1])
         interleave(nc.scalar.copy, 1, 0, 0, 512)
         move_scales(0, nc.sync, every)
         later = byte_tile("later_weights", 28 * N, "raw10")
@@ -239,8 +239,11 @@ def tile_moe_eps_lin_relu2_kernel(tc, xT, w_words, w_scales, b, offs, out):
         load_weight_words(later[:, 4 * N : 12 * N], [2, 3], range(4))
         load_weight_words(later[:, 12 * N : 20 * N], range(4, E), [0, 1])
         load_weight_words(later[:, 20 * N :], range(4, E), [2, 3])
-        interleave(nc.scalar.copy, 1, 1, 0, 512)
+        interleave(nc.scalar.copy, 1, 1, 0, 384)
+        interleave(nc.gpsimd.tensor_copy, 1, 1, 384, 512)
         quantize(1, 0)
+        word_tile(0, range(5, E), 1, "grouped10")
+        gather_words(0, range(5, E), [1])
         word_tile(1, range(3), 0)
         gather_words(1, range(3), [0])
         quantize(1, 1)
@@ -254,12 +257,18 @@ def tile_moe_eps_lin_relu2_kernel(tc, xT, w_words, w_scales, b, offs, out):
         gather_words(1, range(4), [1])
         gather_words(1, range(4, E), [1, 0])
 
-        finish(multiply(0, [0], range(4)), "g")
+        for tiles in ([0, 1], [2, 3]):
+            rectify(multiply(0, [0], tiles))
+        square("g", 0, [0], range(4))
         finish(multiply(0, [1], range(4)), "g")
         finish(multiply(0, [2, 3], [0, 1]), "g")
         finish(multiply(0, [2, 3], [2, 3]), "g")
         low, high = range(4), range(4, E)
-        for t, engine in enumerate("ssg"):
+        for pair in ([4, 5], [6, 7]):
+            rectify(multiply(0, pair, [0]))
+        square("s", 0, high, [0])
+        store(0, 0)
+        for t, engine in ((1, "s"), (2, "g")):
             finish(multiply(0, high, [t]), engine)
             store(0, t)
         waiting = multiply(0, high, [3])
@@ -271,7 +280,7 @@ def tile_moe_eps_lin_relu2_kernel(tc, xT, w_words, w_scales, b, offs, out):
         early.append(multiply(1, low, [2]))
         for e in (6, 7):
             add_bias(multiply(1, [e], [0]))
-        square("v", 1, [6, 7], [0])
+            square("v", 1, [e], [0])
         store(1, 0)
         for t in (1, 2):
             finish(early[t - 1], "s")

@@ -27,10 +27,11 @@ def tile_moe_eps_lin_relu2_kernel(tc, xT, w_words, w_scales, b, offs, out):
     nc = tc.nc
     with ExitStack() as ctx:
         keep = ctx.enter_context(tc.tile_pool(name="keep", bufs=1))
+        shared = ctx.enter_context(tc.tile_pool(name="shared", bufs=1))
         psum = ctx.enter_context(tc.psum_pool(name="psum", bufs=8))
 
         offsets = keep.tile([P, E * C // 16], U16, name="offsets")
-        raw = [[keep.tile([P, 4, HALF], F32, align_bytes=256, name=f"raw{h}{a}") for a in range(2)] for h in range(2)]
+        raw = {}
         grouped = [[keep.tile([P, HALF, 4], BF16, align_bytes=256, name=f"grouped{h}{a}") for a in range(2)] for h in range(2)]
         words = [keep.tile([P, T], U32, align_bytes=256, name=f"words{a}") for a in range(2)]
         scales = keep.tile([P, T], U8, align_bytes=256, name="scales")
@@ -42,9 +43,12 @@ def tile_moe_eps_lin_relu2_kernel(tc, xT, w_words, w_scales, b, offs, out):
         ww = {}
         ws = {}
 
-        def load_x(h, a, lo=0, hi=HALF):
+        def load_x(h, a, lo=0, hi=HALF, tile=None):
+            if tile is None:
+                tile = keep.tile([P, 4, hi - lo], F32, align_bytes=256, name=f"raw{h}{a}_{lo}")
+            raw[h, a, lo] = tile
             rows = xT[512 * a : 512 * (a + 1), HALF * h + lo : HALF * h + hi]
-            nc.sync.dma_start(raw[h][a][:, :, lo:hi], rows.rearrange("(p j) w -> p j w", j=4))
+            nc.sync.dma_start(raw[h, a, lo][:], rows.rearrange("(p j) w -> p j w", j=4))
 
         def load_weight_scales(queue, tile, experts):
             lo, n = experts[0], len(experts)
@@ -74,10 +78,10 @@ def tile_moe_eps_lin_relu2_kernel(tc, xT, w_words, w_scales, b, offs, out):
             held["bias"] = keep.tile([P, N // P, E], F32, align_bytes=256, name="bias", tag=tag)
             queue.dma_start(held["bias"][:], b.rearrange("(t p) e -> p t e", p=P))
 
-        def interleave(copy, h, a, lo, hi):
+        def interleave(copy, h, a, lo, hi, base=0):
             copy(
                 out=grouped[h][a][:, lo:hi, :].rearrange("p (g i) j -> p g j i", i=4),
-                in_=raw[h][a][:, :, lo:hi].rearrange("p j (g i) -> p g j i", i=4),
+                in_=raw[h, a, base][:, :, lo - base : hi - base].rearrange("p j (g i) -> p g j i", i=4),
             )
 
         def quantize(h, a, lo=0, hi=HALF):
@@ -93,9 +97,10 @@ def tile_moe_eps_lin_relu2_kernel(tc, xT, w_words, w_scales, b, offs, out):
             window = table[:, : HALF * (h + 1)]
             nc.vector.tensor_copy(target, window.indirect(offsets[:, first : first + P // 16]))
 
-        def word_tile(h, experts, a, tag=None):
+        def word_tile(h, experts, a, tag=None, tile=None):
             name = f"slot_words{h}{experts[0]}{a}"
-            tile = keep.tile([P, len(experts) * P], U32, align_bytes=256, name=name, tag=tag or name)
+            if tile is None:
+                tile = keep.tile([P, len(experts) * P], U32, align_bytes=256, name=name, tag=tag or name)
             for i, e in enumerate(experts):
                 slot_words[h, e, a] = tile[:, P * i : P * (i + 1)]
 
@@ -212,29 +217,34 @@ def tile_moe_eps_lin_relu2_kernel(tc, xT, w_words, w_scales, b, offs, out):
         nc.sync.dma_start(offsets[:], offs)
         load_x(0, 1, 0, 256)
         load_x(0, 1, 256, 512)
-        load_x(1, 0)
+        load_x(1, 0, tile=shared.tile([P, 4, HALF], F32, align_bytes=256, name="raw10", offset=0))
         load_x(1, 1)
         load_weight_words(byte_tile("first_weights", 4 * N)[:], [0], range(4))
 
         interleave(nc.vector.tensor_copy, 0, 0, 0, 176)
         interleave(nc.scalar.copy, 0, 0, 176, 256)
         quantize(0, 0, 0, 256)
-        interleave(nc.vector.tensor_copy, 0, 0, 256, 432)
-        interleave(nc.scalar.copy, 0, 0, 432, 512)
-        load_weight_scales(nc.gpsimd, byte_tile("weight_scales", 16 * N, "raw00")[:], every)
-        quantize(0, 0, 256, 512)
+        interleave(nc.vector.tensor_copy, 0, 0, 256, 384, 256)
+        interleave(nc.vector.tensor_copy, 0, 0, 384, 432, 256)
+        interleave(nc.scalar.copy, 0, 0, 432, 512, 256)
+        load_weight_scales(nc.gpsimd, byte_tile("weight_scales", 16 * N, "raw00_256")[:], every)
+        quantize(0, 0, 256, 384)
+        quantize(0, 0, 384, 512)
         load_bias(nc.gpsimd, "grouped00")
-        word_tile(0, every, 0)
-        gather_words(0, every, [0])
+        word_tile(0, range(7), 0)
+        gather_words(0, range(7), [0])
         interleave(nc.scalar.copy, 0, 1, 0, 256)
-        interleave(nc.scalar.copy, 0, 1, 256, 512)
-        quantize(0, 1)
+        interleave(nc.scalar.copy, 0, 1, 256, 512, 256)
+        quantize(0, 1, 0, 256)
+        quantize(0, 1, 256, 512)
+        word_tile(0, [7], 0, "raw01_256")
+        gather_words(0, [7], [0])
         gather_scales(0, every)
-        word_tile(0, range(5), 1)
-        gather_words(0, range(5), [1])
+        word_tile(0, range(6), 1)
+        gather_words(0, range(6), [1])
         interleave(nc.scalar.copy, 1, 0, 0, 512)
         move_scales(0, nc.sync, every)
-        later = byte_tile("later_weights", 28 * N, "raw10")
+        later = shared.tile([P, 28 * N], U8, align_bytes=256, name="later_weights", offset=2 * N)
         load_weight_words(later[:, : 4 * N], [1], range(4))
         load_weight_words(later[:, 4 * N : 12 * N], [2, 3], range(4))
         load_weight_words(later[:, 12 * N : 20 * N], range(4, E), [0, 1])
@@ -242,20 +252,20 @@ def tile_moe_eps_lin_relu2_kernel(tc, xT, w_words, w_scales, b, offs, out):
         interleave(nc.scalar.copy, 1, 1, 0, 384)
         interleave(nc.gpsimd.tensor_copy, 1, 1, 384, 512)
         quantize(1, 0)
-        word_tile(0, range(5, E), 1, "grouped10")
-        gather_words(0, range(5, E), [1])
-        word_tile(1, range(3), 0)
-        gather_words(1, range(3), [0])
+        word_tile(0, [6, 7], 1, tile=shared.tile([P, 2 * P], U32, align_bytes=256, name="slot_words061", offset=0))
+        gather_words(0, [6, 7], [1])
+        word_tile(1, range(4), 0)
+        gather_words(1, range(4), [0])
         quantize(1, 1)
-        word_tile(1, [3], 0, "raw11")
-        gather_words(1, [3], [0])
+        word_tile(1, [4], 0, "raw11_0")
+        gather_words(1, [4], [0])
         for group in (range(4), range(4, E)):
             gather_scales(1, group)
             move_scales(1, nc.sync, group)
-        word_tile(1, range(4, E), 0, "grouped11")
+        word_tile(1, range(5, E), 0, "grouped11")
         word_tile(1, every, 1)
-        gather_words(1, range(4), [1])
-        gather_words(1, range(4, E), [1, 0])
+        gather_words(1, range(5), [1])
+        gather_words(1, range(5, E), [1, 0])
 
         for tiles in ([0, 1], [2, 3]):
             rectify(multiply(0, [0], tiles))

@@ -35,7 +35,7 @@ def tile_moe_eps_lin_relu2_kernel(tc, xT, w_words, w_scales, b, offs, out):
         grouped = [[keep.tile([P, HALF, 4], BF16, align_bytes=256, name=f"grouped{h}{a}") for a in range(2)] for h in range(2)]
         words = [keep.tile([P, T], U32, align_bytes=256, name=f"words{a}") for a in range(2)]
         scales = keep.tile([P, T], U8, align_bytes=256, name="scales")
-        both = [keep.tile([P, E * P], U8, align_bytes=256, name=f"both{h}") for h in range(2)]
+        both = {}
         held = {}
         results = [keep.tile([P, 4, R // 2, E, U], F32, name=f"results{h}") for h in range(2)]
         slot_words = {}
@@ -45,7 +45,7 @@ def tile_moe_eps_lin_relu2_kernel(tc, xT, w_words, w_scales, b, offs, out):
 
         def load_x(h, a, lo=0, hi=HALF, tile=None):
             if tile is None:
-                tile = keep.tile([P, 4, hi - lo], F32, align_bytes=256, name=f"raw{h}{a}_{lo}")
+                tile = keep.tile([P, 4, hi - lo], F32, align_bytes=256, name=f"raw{h}{a}_{lo}", tag=f"raw{h}{a}_{lo}")
             raw[h, a, lo] = tile
             rows = xT[512 * a : 512 * (a + 1), HALF * h + lo : HALF * h + hi]
             nc.sync.dma_start(raw[h, a, lo][:], rows.rearrange("(p j) w -> p j w", j=4))
@@ -74,8 +74,8 @@ def tile_moe_eps_lin_relu2_kernel(tc, xT, w_words, w_scales, b, offs, out):
         def byte_tile(name, width, tag=None):
             return keep.tile([P, width], U8, align_bytes=256, name=name, tag=tag or name)
 
-        def load_bias(queue, tag):
-            held["bias"] = keep.tile([P, N // P, E], F32, align_bytes=256, name="bias", tag=tag)
+        def load_bias(queue, tile):
+            held["bias"] = tile
             queue.dma_start(held["bias"][:], b.rearrange("(t p) e -> p t e", p=P))
 
         def interleave(copy, h, a, lo, hi, base=0):
@@ -109,16 +109,20 @@ def tile_moe_eps_lin_relu2_kernel(tc, xT, w_words, w_scales, b, offs, out):
                 for a in passes:
                     gather(slot_words[h, e, a], words[a], h, e)
 
-        def gather_scales(h, experts):
-            for e in experts:
-                gather(both[h][:, P * e : P * (e + 1)], scales, h, e)
+        def gather_scales(h, experts, tile=None):
+            if tile is None:
+                tile = byte_tile(f"both{h}{experts[0]}", len(experts) * P)
+            for i, e in enumerate(experts):
+                both[h, e] = tile[:, P * i : P * (i + 1)]
+                gather(both[h, e], scales, h, e)
+            both[h, experts[0], "all"] = tile
 
-        def move_scales(h, queue, experts, tag=None):
+        def move_scales(h, queue, experts, tile=None):
             lo, n = experts[0], len(experts)
-            name = f"second{h}{lo}"
-            tile = keep.tile([P, n * P], U8, align_bytes=256, name=name, tag=tag or name)
+            if tile is None:
+                tile = keep.tile([P, n * P], U8, align_bytes=256, name=f"second{h}{lo}")
             for r in range(4):
-                queue.dma_start(tile[r:P:32, :].bitcast(I32), both[h][r + 4 : P : 32, P * lo : P * (lo + n)].bitcast(I32))
+                queue.dma_start(tile[r:P:32, :].bitcast(I32), both[h, lo, "all"][r + 4 : P : 32, :].bitcast(I32))
             for e in experts:
                 second[h, e] = tile[:, P * (e - lo) : P * (e - lo + 1)]
 
@@ -128,7 +132,7 @@ def tile_moe_eps_lin_relu2_kernel(tc, xT, w_words, w_scales, b, offs, out):
                 lhsT=ww[e, a, t].bitcast(FP4X4),
                 lhsT_scale=ws[e][:, N * a + P * t : N * a + P * (t + 1)],
                 rhs=slot_words[h, e, a].bitcast(FP8X4),
-                rhs_scale=second[h, e] if a == 1 else both[h][:, P * e : P * (e + 1)],
+                rhs_scale=second[h, e] if a == 1 else both[h, e],
                 start=start,
                 stop=stop,
             )
@@ -140,17 +144,6 @@ def tile_moe_eps_lin_relu2_kernel(tc, xT, w_words, w_scales, b, offs, out):
                     product(bank[:, i, j, :], h, e, t, 1, True, False)
                     product(bank[:, i, j, :], h, e, t, 0, False, True)
             return bank, h, experts, tiles
-
-        def multiply_by_passes(h, experts, tile_sets):
-            banks = [psum.tile([P, len(experts), len(tiles), P], F32, name="bank") for tiles in tile_sets]
-            for a in range(2):
-                for bank, tiles in zip(banks, tile_sets):
-                    for i, e in enumerate(experts):
-                        for j, t in enumerate(tiles):
-                            first = a == 0 and i == 0 and j == 0
-                            last = a == 1 and i == len(experts) - 1 and j == len(tiles) - 1
-                            product(bank[:, i, j, :], h, e, t, a, first, last)
-            return [(bank, h, experts, tiles) for bank, tiles in zip(banks, tile_sets)]
 
         def rectify(job):
             bank, h, experts, tiles = job
@@ -183,16 +176,6 @@ def tile_moe_eps_lin_relu2_kernel(tc, xT, w_words, w_scales, b, offs, out):
             else:
                 nc.gpsimd.tensor_tensor(v, v, v, MULT)
 
-        def vector_pass(job, t, second_step):
-            bank, h, experts, tiles = job
-            sums = bank[:, 0, tiles.index(t), :].rearrange("p (m u) -> p m u", u=U)
-            target = results[h][:, t, :, experts[0], :]
-            column = held["bias"][:, t, experts[0] : experts[0] + 1]
-            if second_step:
-                nc.vector.scalar_tensor_tensor(target, sums, column, target, ADD, MULT)
-            else:
-                nc.vector.tensor_scalar(target, sums, column, 0.0, ADD, MAX)
-
         def finish(job, engine):
             rectify(job)
             square(engine, job[1], job[2], job[3])
@@ -209,7 +192,7 @@ def tile_moe_eps_lin_relu2_kernel(tc, xT, w_words, w_scales, b, offs, out):
             rows = out[P * t : P * (t + 1), T * h : T * (h + 1)]
             nc.sync.dma_start(rows, results[h][:, t].rearrange("p m e u -> p (m e u)"))
 
-        every = range(E)
+        every, low, high = range(E), range(4), range(4, E)
         nc.gpsimd.memset(scales[:].bitcast(I32), 0)
 
         load_x(0, 0, 0, 256)
@@ -230,7 +213,7 @@ def tile_moe_eps_lin_relu2_kernel(tc, xT, w_words, w_scales, b, offs, out):
         load_weight_scales(nc.gpsimd, byte_tile("weight_scales", 16 * N, "raw00_256")[:], every)
         quantize(0, 0, 256, 384)
         quantize(0, 0, 384, 512)
-        load_bias(nc.gpsimd, "grouped00")
+        load_bias(nc.gpsimd, keep.tile([P, N // P, E], F32, align_bytes=256, name="bias", tag="grouped00"))
         word_tile(0, range(7), 0)
         gather_words(0, range(7), [0])
         interleave(nc.scalar.copy, 0, 1, 0, 256)
@@ -249,23 +232,19 @@ def tile_moe_eps_lin_relu2_kernel(tc, xT, w_words, w_scales, b, offs, out):
         load_weight_words(later[:, 4 * N : 12 * N], [2, 3], range(4))
         load_weight_words(later[:, 12 * N : 20 * N], range(4, E), [0, 1])
         load_weight_words(later[:, 20 * N :], range(4, E), [2, 3])
-        interleave(nc.scalar.copy, 1, 1, 0, 384)
-        interleave(nc.gpsimd.tensor_copy, 1, 1, 384, 512)
+        interleave(nc.scalar.copy, 1, 1, 0, 512)
         quantize(1, 0)
         word_tile(0, [6, 7], 1, tile=shared.tile([P, 2 * P], U32, align_bytes=256, name="slot_words061", offset=0))
         gather_words(0, [6, 7], [1])
-        word_tile(1, range(4), 0)
-        gather_words(1, range(4), [0])
         quantize(1, 1)
-        word_tile(1, [4], 0, "raw11_0")
-        gather_words(1, [4], [0])
-        for group in (range(4), range(4, E)):
-            gather_scales(1, group)
-            move_scales(1, nc.sync, group)
-        word_tile(1, range(5, E), 0, "grouped11")
+        word_tile(1, [0], 0, "raw11_0")
+        gather_words(1, [0], [0])
+        gather_scales(1, every)
+        move_scales(1, nc.sync, every)
+        word_tile(1, range(1, E), 0, "grouped11")
         word_tile(1, every, 1)
-        gather_words(1, range(5), [1])
-        gather_words(1, range(5, E), [1, 0])
+        gather_words(1, [0], [1])
+        gather_words(1, range(1, E), [1, 0])
 
         for tiles in ([0, 1], [2, 3]):
             rectify(multiply(0, [0], tiles))
@@ -273,10 +252,10 @@ def tile_moe_eps_lin_relu2_kernel(tc, xT, w_words, w_scales, b, offs, out):
         finish(multiply(0, [1], range(4)), "g")
         finish(multiply(0, [2, 3], [0, 1]), "g")
         finish(multiply(0, [2, 3], [2, 3]), "g")
-        low, high = range(4), range(4, E)
         for pair in ([4, 5], [6, 7]):
             rectify(multiply(0, pair, [0]))
-        square("s", 0, high, [0])
+        for pair in ([4, 5], [6, 7]):
+            square("s", 0, pair, [0])
         store(0, 0)
         for t, engine in ((1, "s"), (2, "g")):
             finish(multiply(0, high, [t]), engine)

@@ -28,7 +28,7 @@ def tile_moe_eps_lin_relu2_kernel(tc, xT, w_words, w_scales, b, offs, out):
     with ExitStack() as ctx:
         keep = ctx.enter_context(tc.tile_pool(name="keep", bufs=1))
         shared = ctx.enter_context(tc.tile_pool(name="shared", bufs=1))
-        psum = ctx.enter_context(tc.psum_pool(name="psum", bufs=8))
+        psum = ctx.enter_context(tc.psum_pool(name="psum", bufs=1))
 
         offsets = keep.tile([P, E * C // 16], U16, name="offsets")
         raw = {}
@@ -137,12 +137,27 @@ def tile_moe_eps_lin_relu2_kernel(tc, xT, w_words, w_scales, b, offs, out):
                 stop=stop,
             )
 
-        def multiply(h, experts, tiles):
-            bank = psum.tile([P, len(experts), len(tiles), P], F32, name="bank")
-            for i, e in enumerate(experts):
+        def new_bank(place, h, experts, tiles):
+            bank = psum.tile([P, len(experts), len(tiles), P], F32, name="bank", tag=f"bank{place}")
+            return bank, h, experts, tiles
+
+        def fill(job, some):
+            bank, h, experts, tiles = job
+            for e in some:
                 for j, t in enumerate(tiles):
-                    product(bank[:, i, j, :], h, e, t, 1, True, False)
-                    product(bank[:, i, j, :], h, e, t, 0, False, True)
+                    product(bank[:, experts.index(e), j, :], h, e, t, 1, True, False)
+                    product(bank[:, experts.index(e), j, :], h, e, t, 0, False, True)
+            return job
+
+        def multiply(place, h, experts, tiles):
+            return fill(new_bank(place, h, experts, tiles), experts)
+
+        def multiply_by_passes(place, h, experts, tiles):
+            bank = new_bank(place, h, experts, tiles)[0]
+            sums = [(i, e, j, t) for i, e in enumerate(experts) for j, t in enumerate(tiles)]
+            for a in range(2):
+                for n, (i, e, j, t) in enumerate(sums):
+                    product(bank[:, i, j, :], h, e, t, a, a == 0 and n == 0, a == 1 and n == len(sums) - 1)
             return bank, h, experts, tiles
 
         def rectify(job):
@@ -182,7 +197,7 @@ def tile_moe_eps_lin_relu2_kernel(tc, xT, w_words, w_scales, b, offs, out):
 
         def finish_on_vector(job):
             bank, h, experts, tiles = job
-            pairs = [(bank[:, i : i + 2], h, experts[i : i + 2], tiles) for i in range(0, len(experts), 2)]
+            pairs = [(bank[:, i : min(i + 2, len(experts))], h, experts[i : i + 2], tiles) for i in range(0, len(experts), 2)]
             for pair in pairs:
                 add_bias(pair)
             for pair in pairs:
@@ -236,45 +251,50 @@ def tile_moe_eps_lin_relu2_kernel(tc, xT, w_words, w_scales, b, offs, out):
         quantize(1, 0)
         word_tile(0, [6, 7], 1, tile=shared.tile([P, 2 * P], U32, align_bytes=256, name="slot_words061", offset=0))
         gather_words(0, [6, 7], [1])
-        quantize(1, 1)
-        word_tile(1, [0], 0, "raw11_0")
+        word_tile(1, [0], 0)
         gather_words(1, [0], [0])
-        gather_scales(1, every)
-        move_scales(1, nc.sync, every)
-        word_tile(1, range(1, E), 0, "grouped11")
+        quantize(1, 1)
+        word_tile(1, [1], 0, "raw11_0")
+        gather_words(1, [1], [0])
+        for group in (low, high):
+            gather_scales(1, group)
+            move_scales(1, nc.sync, group)
+        word_tile(1, range(2, E), 0, "grouped11")
         word_tile(1, every, 1)
-        gather_words(1, [0], [1])
-        gather_words(1, range(1, E), [1, 0])
+        gather_words(1, [0, 1], [1])
+        gather_words(1, range(2, E), [1, 0])
 
-        for tiles in ([0, 1], [2, 3]):
-            rectify(multiply(0, [0], tiles))
-        square("g", 0, [0], range(4))
-        finish(multiply(0, [1], range(4)), "g")
-        finish(multiply(0, [2, 3], [0, 1]), "g")
-        finish(multiply(0, [2, 3], [2, 3]), "g")
-        for pair in ([4, 5], [6, 7]):
-            rectify(multiply(0, pair, [0]))
+        finish(multiply_by_passes(0, 0, [0], range(4)), "g")
+        finish(multiply(1, 0, [1], range(4)), "g")
+        finish(multiply(2, 0, [2, 3], [0, 1]), "g")
+        finish(multiply(3, 0, [2, 3], [2, 3]), "g")
+        for place, pair in ((4, [4, 5]), (5, [6, 7])):
+            rectify(multiply(place, 0, pair, [0]))
         for pair in ([4, 5], [6, 7]):
             square("s", 0, pair, [0])
         store(0, 0)
-        for t, engine in ((1, "s"), (2, "g")):
-            finish(multiply(0, high, [t]), engine)
+        for place, t, engine in ((6, 1, "s"), (7, 2, "g")):
+            finish(multiply(place, 0, high, [t]), engine)
             store(0, t)
-        waiting = multiply(0, high, [3])
-        finish(multiply(1, low, [0]), "g")
+        waiting = multiply(0, 0, high, [3])
+        finish(multiply(1, 1, low, [0]), "g")
         finish(waiting, "s")
         store(0, 3)
-        early = [multiply(1, low, [1])]
-        finish(multiply(1, [4, 5], [0]), "s")
-        early.append(multiply(1, low, [2]))
-        for e in (6, 7):
-            add_bias(multiply(1, [e], [0]))
+        early = [multiply(2, 1, low, [1])]
+        finish(multiply(3, 1, [4, 5], [0]), "s")
+        early.append(multiply(4, 1, low, [2]))
+        second_tile = fill(new_bank(5, 1, high, [1]), [4, 5])
+        for place, e in ((6, 6), (7, 7)):
+            add_bias(multiply(place, 1, [e], [0]))
+            fill(second_tile, [e])
             square("v", 1, [e], [0])
         store(1, 0)
-        for t in (1, 2):
-            finish(early[t - 1], "s")
-            finish_on_vector(multiply(1, high, [t]))
-            store(1, t)
-        finish(multiply(1, low, [3]), "s")
-        finish_on_vector(multiply(1, high, [3]))
+        finish(early[0], "s")
+        finish_on_vector(second_tile)
+        store(1, 1)
+        finish(early[1], "s")
+        finish_on_vector(multiply(0, 1, high, [2]))
+        store(1, 2)
+        finish(multiply(1, 1, low, [3]), "s")
+        finish_on_vector(multiply(3, 1, high, [3]))
         store(1, 3)

@@ -210,8 +210,8 @@ def tile_moe_eps_lin_relu2_kernel(tc, xT, w_words, w_scales, b, offs, out):
         every, low, high = range(E), range(4), range(4, E)
         nc.gpsimd.memset(scales[:].bitcast(I32), 0)
 
-        load_x(0, 0, 0, 256)
-        load_x(0, 0, 256, 512)
+        load_x(0, 0, 0, 384)
+        load_x(0, 0, 384, 512)
         nc.sync.dma_start(offsets[:], offs)
         load_x(0, 1, 0, 256)
         load_x(0, 1, 256, 512)
@@ -219,13 +219,14 @@ def tile_moe_eps_lin_relu2_kernel(tc, xT, w_words, w_scales, b, offs, out):
         load_x(1, 1)
         load_weight_words(byte_tile("first_weights", 4 * N)[:], [0], range(4))
 
-        interleave(nc.vector.tensor_copy, 0, 0, 0, 176)
-        interleave(nc.scalar.copy, 0, 0, 176, 256)
-        quantize(0, 0, 0, 256)
-        interleave(nc.vector.tensor_copy, 0, 0, 256, 384, 256)
-        interleave(nc.vector.tensor_copy, 0, 0, 384, 432, 256)
-        interleave(nc.scalar.copy, 0, 0, 432, 512, 256)
-        load_weight_scales(nc.gpsimd, byte_tile("weight_scales", 16 * N, "raw00_256")[:], every)
+        interleave(nc.vector.tensor_copy, 0, 0, 0, 128)
+        interleave(nc.vector.tensor_copy, 0, 0, 128, 256)
+        interleave(nc.scalar.copy, 0, 0, 256, 384)
+        quantize(0, 0, 0, 128)
+        quantize(0, 0, 128, 256)
+        interleave(nc.vector.tensor_copy, 0, 0, 384, 464, 384)
+        interleave(nc.scalar.copy, 0, 0, 464, 512, 384)
+        load_weight_scales(nc.gpsimd, byte_tile("weight_scales", 16 * N, "raw00_384")[:], every)
         quantize(0, 0, 256, 384)
         quantize(0, 0, 384, 512)
         load_bias(nc.gpsimd, keep.tile([P, N // P, E], F32, align_bytes=256, name="bias", tag="grouped00"))
@@ -282,13 +283,13 @@ def tile_moe_eps_lin_relu2_kernel(tc, xT, w_words, w_scales, b, offs, out):
         store(0, 3)
         early = [multiply(2, 1, low, [1])]
         finish(multiply(3, 1, [4, 5], [0]), "s")
-        early.append(multiply(4, 1, low, [2]))
         second_tile = fill(new_bank(5, 1, high, [1]), [4, 5])
         for place, e in ((6, 6), (7, 7)):
             add_bias(multiply(place, 1, [e], [0]))
             fill(second_tile, [e])
             square("v", 1, [e], [0])
         store(1, 0)
+        early.append(multiply(4, 1, low, [2]))
         finish(early[0], "s")
         finish_on_vector(second_tile)
         store(1, 1)

@@ -233,7 +233,8 @@ def tile_moe_eps_lin_relu2_kernel(tc, xT, w_words, w_scales, b, offs, out):
         word_tile(0, range(7), 0)
         gather_words(0, range(7), [0])
         interleave(nc.scalar.copy, 0, 1, 0, 256)
-        interleave(nc.scalar.copy, 0, 1, 256, 512, 256)
+        interleave(nc.scalar.copy, 0, 1, 256, 384, 256)
+        interleave(nc.vector.tensor_copy, 0, 1, 384, 512, 256)
         quantize(0, 1, 0, 256)
         quantize(0, 1, 256, 512)
         word_tile(0, [7], 0, "raw01_256")
@@ -252,18 +253,18 @@ def tile_moe_eps_lin_relu2_kernel(tc, xT, w_words, w_scales, b, offs, out):
         quantize(1, 0)
         word_tile(0, [6, 7], 1, tile=shared.tile([P, 2 * P], U32, align_bytes=256, name="slot_words061", offset=0))
         gather_words(0, [6, 7], [1])
-        word_tile(1, [0], 0)
-        gather_words(1, [0], [0])
+        word_tile(1, range(2), 0)
+        gather_words(1, range(2), [0])
         quantize(1, 1)
-        word_tile(1, [1], 0, "raw11_0")
-        gather_words(1, [1], [0])
+        word_tile(1, [2], 0, "raw11_0")
+        gather_words(1, [2], [0])
         for group in (low, high):
             gather_scales(1, group)
             move_scales(1, nc.sync, group)
-        word_tile(1, range(2, E), 0, "grouped11")
+        word_tile(1, range(3, E), 0, "grouped11")
         word_tile(1, every, 1)
-        gather_words(1, [0, 1], [1])
-        gather_words(1, range(2, E), [1, 0])
+        gather_words(1, range(3), [1])
+        gather_words(1, range(3, E), [1, 0])
 
         finish(multiply_by_passes(0, 0, [0], range(4)), "g")
         finish(multiply(1, 0, [1], range(4)), "g")
@@ -283,13 +284,13 @@ def tile_moe_eps_lin_relu2_kernel(tc, xT, w_words, w_scales, b, offs, out):
         store(0, 3)
         early = [multiply(2, 1, low, [1])]
         finish(multiply(3, 1, [4, 5], [0]), "s")
+        early.append(multiply(4, 1, low, [2]))
         second_tile = fill(new_bank(5, 1, high, [1]), [4, 5])
         for place, e in ((6, 6), (7, 7)):
             add_bias(multiply(place, 1, [e], [0]))
             fill(second_tile, [e])
             square("v", 1, [e], [0])
         store(1, 0)
-        early.append(multiply(4, 1, low, [2]))
         finish(early[0], "s")
         finish_on_vector(second_tile)
         store(1, 1)

@@ -275,22 +275,26 @@ def tile_moe_eps_lin_relu2_kernel(tc, xT, w_words, w_scales, b, offs, out):
         for pair in ([4, 5], [6, 7]):
             square("s", 0, pair, [0])
         store(0, 0)
-        for place, t, engine in ((6, 1, "s"), (7, 2, "g")):
-            finish(multiply(place, 0, high, [t]), engine)
+        finish(multiply(6, 0, high, [1]), "s")
+        store(0, 1)
+        for place, t in ((7, 2), (0, 3)):
+            rectify(multiply(place, 0, high, [t]))
+            square("g", 0, [4, 5], [t])
+            square("s", 0, [6, 7], [t])
             store(0, t)
-        waiting = multiply(0, 0, high, [3])
-        finish(multiply(1, 1, low, [0]), "g")
-        finish(waiting, "s")
-        store(0, 3)
+        finish(multiply(1, 1, low, [0]), "s")
         early = [multiply(2, 1, low, [1])]
-        finish(multiply(3, 1, [4, 5], [0]), "s")
-        early.append(multiply(4, 1, low, [2]))
+        first = [multiply(3, 1, [4, 5], [0])]
         second_tile = fill(new_bank(5, 1, high, [1]), [4, 5])
         for place, e in ((6, 6), (7, 7)):
-            add_bias(multiply(place, 1, [e], [0]))
+            first.append(multiply(place, 1, [e], [0]))
             fill(second_tile, [e])
-            square("v", 1, [e], [0])
+        for job in first:
+            add_bias(job)
+        for job in first:
+            square("v", 1, job[2], [0])
         store(1, 0)
+        early.append(multiply(4, 1, low, [2]))
         finish(early[0], "s")
         finish_on_vector(second_tile)
         store(1, 1)

@@ -152,20 +152,19 @@ def tile_moe_eps_lin_relu2_kernel(tc, xT, w_words, w_scales, b, offs, out):
         def multiply(place, h, experts, tiles):
             return fill(new_bank(place, h, experts, tiles), experts)
 
-        def multiply_by_passes(place, h, experts, tiles):
-            bank = new_bank(place, h, experts, tiles)[0]
+        def one_pass(job, a):
+            bank, h, experts, tiles = job
             sums = [(i, e, j, t) for i, e in enumerate(experts) for j, t in enumerate(tiles)]
-            for a in range(2):
-                for n, (i, e, j, t) in enumerate(sums):
-                    product(bank[:, i, j, :], h, e, t, a, a == 0 and n == 0, a == 1 and n == len(sums) - 1)
-            return bank, h, experts, tiles
+            for n, (i, e, j, t) in enumerate(sums):
+                product(bank[:, i, j, :], h, e, t, a, a == 0 and n == 0, a == 1 and n == len(sums) - 1)
 
-        def rectify(job):
+        def rectify(job, only=None, stage=None):
             bank, h, experts, tiles = job
             for j, t in enumerate(tiles):
-                for i, e in enumerate(experts):
+                for i, e in enumerate(experts if only in (None, t) else []):
                     sums = bank[:, i, j, :].rearrange("p (m u) -> p m u", u=U)
-                    nc.scalar.activation(results[h][:, t, :, e, :], sums, RELU, bias=held["bias"][:, t, e : e + 1])
+                    target = results[h][:, t, :, e, :] if stage is None else stage[:, :, i, :]
+                    nc.scalar.activation(target, sums, RELU, bias=held["bias"][:, t, e : e + 1])
 
         def add_bias(job):
             bank, h, experts, tiles = job
@@ -203,6 +202,22 @@ def tile_moe_eps_lin_relu2_kernel(tc, xT, w_words, w_scales, b, offs, out):
             for pair in pairs:
                 square("v", h, pair[2], tiles)
 
+        def parts(job):
+            bank, h, experts, tiles = job
+            return [
+                (results[h][:, t, :, e, :], bank[:, i, j, :].rearrange("p (m u) -> p m u", u=U), held["bias"][:, t, e : e + 1])
+                for i, e in enumerate(experts)
+                for j, t in enumerate(tiles)
+            ]
+
+        def rectify_on_vector(job):
+            for target, sums, column in parts(job):
+                nc.vector.tensor_scalar(target, sums, column, 0.0, ADD, MAX)
+
+        def square_on_vector(job):
+            for target, sums, column in parts(job):
+                nc.vector.scalar_tensor_tensor(target, sums, column, target, ADD, MULT)
+
         def store(h, t):
             rows = out[P * t : P * (t + 1), T * h : T * (h + 1)]
             nc.sync.dma_start(rows, results[h][:, t].rearrange("p m e u -> p (m e u)"))
@@ -217,7 +232,8 @@ def tile_moe_eps_lin_relu2_kernel(tc, xT, w_words, w_scales, b, offs, out):
         load_x(0, 1, 256, 512)
         load_x(1, 0, tile=shared.tile([P, 4, HALF], F32, align_bytes=256, name="raw10", offset=0))
         load_x(1, 1)
-        load_weight_words(byte_tile("first_weights", 4 * N)[:], [0], range(4))
+        for e in (0, 1):
+            load_weight_words(byte_tile(f"first_weights{e}", 4 * N)[:], [e], range(4))
 
         interleave(nc.vector.tensor_copy, 0, 0, 0, 128)
         interleave(nc.vector.tensor_copy, 0, 0, 128, 256)
@@ -230,77 +246,94 @@ def tile_moe_eps_lin_relu2_kernel(tc, xT, w_words, w_scales, b, offs, out):
         quantize(0, 0, 256, 384)
         quantize(0, 0, 384, 512)
         load_bias(nc.gpsimd, keep.tile([P, N // P, E], F32, align_bytes=256, name="bias", tag="grouped00"))
-        word_tile(0, range(7), 0)
-        gather_words(0, range(7), [0])
+        word_tile(0, every, 0)
+        gather_words(0, every, [0])
         interleave(nc.scalar.copy, 0, 1, 0, 256)
         interleave(nc.scalar.copy, 0, 1, 256, 384, 256)
         interleave(nc.vector.tensor_copy, 0, 1, 384, 512, 256)
         quantize(0, 1, 0, 256)
         quantize(0, 1, 256, 512)
-        word_tile(0, [7], 0, "raw01_256")
-        gather_words(0, [7], [0])
         gather_scales(0, every)
-        word_tile(0, range(6), 1)
-        gather_words(0, range(6), [1])
+        word_tile(0, every, 1)
+        gather_words(0, every, [1])
         interleave(nc.scalar.copy, 1, 0, 0, 512)
         move_scales(0, nc.sync, every)
-        later = shared.tile([P, 28 * N], U8, align_bytes=256, name="later_weights", offset=2 * N)
-        load_weight_words(later[:, : 4 * N], [1], range(4))
-        load_weight_words(later[:, 4 * N : 12 * N], [2, 3], range(4))
-        load_weight_words(later[:, 12 * N : 20 * N], range(4, E), [0, 1])
-        load_weight_words(later[:, 20 * N :], range(4, E), [2, 3])
+        later = shared.tile([P, 24 * N], U8, align_bytes=256, name="later_weights", offset=0)
+        load_weight_words(later[:, : 4 * N], [2], range(4))
+        load_weight_words(later[:, 4 * N : 8 * N], [3], range(4))
+        load_weight_words(later[:, 8 * N : 12 * N], [4, 5], [0, 1])
+        load_weight_words(later[:, 12 * N : 16 * N], [6, 7], [0, 1])
+        load_weight_words(later[:, 16 * N : 20 * N], [4, 5], [2, 3])
+        load_weight_words(later[:, 20 * N :], [6, 7], [2, 3])
         interleave(nc.scalar.copy, 1, 1, 0, 512)
         quantize(1, 0)
-        word_tile(0, [6, 7], 1, tile=shared.tile([P, 2 * P], U32, align_bytes=256, name="slot_words061", offset=0))
-        gather_words(0, [6, 7], [1])
-        word_tile(1, range(2), 0)
-        gather_words(1, range(2), [0])
+        word_tile(1, range(3), 0)
+        gather_words(1, range(3), [0])
         quantize(1, 1)
-        word_tile(1, [2], 0, "raw11_0")
-        gather_words(1, [2], [0])
-        for group in (low, high):
-            gather_scales(1, group)
-            move_scales(1, nc.sync, group)
+        gather_scales(1, every)
+        move_scales(1, nc.sync, every)
         word_tile(1, range(3, E), 0, "grouped11")
         word_tile(1, every, 1)
-        gather_words(1, range(3), [1])
-        gather_words(1, range(3, E), [1, 0])
+        gather_words(1, [3], [0])
+        gather_words(1, low, [1])
+        gather_words(1, high, [1, 0])
 
-        finish(multiply_by_passes(0, 0, [0], range(4)), "g")
-        finish(multiply(1, 0, [1], range(4)), "g")
-        finish(multiply(2, 0, [2, 3], [0, 1]), "g")
-        finish(multiply(3, 0, [2, 3], [2, 3]), "g")
-        for place, pair in ((4, [4, 5]), (5, [6, 7])):
-            rectify(multiply(place, 0, pair, [0]))
-        for pair in ([4, 5], [6, 7]):
-            square("s", 0, pair, [0])
+        opening = [new_bank(e, 0, [e], range(4)) for e in (0, 1)]
+        for a in range(2):
+            for job in opening:
+                one_pass(job, a)
+        for job in opening:
+            rectify(job)
+        square("g", 0, [0, 1], [0, 1])
+        for e in (2, 3):
+            rectify(multiply(e, 0, [e], range(4)))
+        square("g", 0, [2, 3], [0, 1])
+        for t in (2, 3):
+            square("g", 0, low, [t])
+        middle = multiply(4, 0, [4, 5], [0, 1])
+        rectify(middle, 0)
+        square("s", 0, [4, 5], [0])
+        finish(multiply(5, 0, [6, 7], [0]), "s")
         store(0, 0)
-        finish(multiply(6, 0, high, [1]), "s")
+        rectify(middle, 1)
+        rectify(multiply(6, 0, [6, 7], [1]))
+        square("s", 0, high, [1])
         store(0, 1)
-        for place, t in ((7, 2), (0, 3)):
-            rectify(multiply(place, 0, high, [t]))
-            square("g", 0, [4, 5], [t])
-            square("s", 0, [6, 7], [t])
-            store(0, t)
-        finish(multiply(1, 1, low, [0]), "s")
-        early = [multiply(2, 1, low, [1])]
-        first = [multiply(3, 1, [4, 5], [0])]
-        second_tile = fill(new_bank(5, 1, high, [1]), [4, 5])
-        for place, e in ((6, 6), (7, 7)):
-            first.append(multiply(place, 1, [e], [0]))
-            fill(second_tile, [e])
-        for job in first:
-            add_bias(job)
-        for job in first:
-            square("v", 1, job[2], [0])
+        middle = multiply(7, 0, [4, 5], [2, 3])
+        rectify(middle, 2)
+        rectify(multiply(0, 0, [6, 7], [2]))
+        square("s", 0, high, [2])
+        store(0, 2)
+        rectify(middle, 3)
+        square("g", 0, [4, 5], [3])
+        finish(multiply(1, 0, [6, 7], [3]), "s")
+        store(0, 3)
+        right_low = [new_bank(place, 1, low, [t]) for t, place in enumerate((5, 4, 6))]
+        for job in right_low:
+            one_pass(job, 0)
+        for job in right_low[:2]:
+            one_pass(job, 1)
+        finish(right_low[0], "g")
+        finish(multiply(2, 1, [4, 5], [0]), "s")
+        waiting = [multiply(3, 1, [6], [0]), multiply(0, 1, [4, 5], [1]), multiply(7, 1, [7], [0])]
+        for job in waiting:
+            rectify_on_vector(job)
+        for job in (waiting[0], waiting[2]):
+            square_on_vector(job)
         store(1, 0)
-        early.append(multiply(4, 1, low, [2]))
-        finish(early[0], "s")
-        finish_on_vector(second_tile)
+        finish(right_low[1], "g")
+        one_pass(right_low[2], 1)
+        rest = multiply(1, 1, [6, 7], [1])
+        rectify_on_vector(rest)
+        for job in (waiting[1], rest):
+            square_on_vector(job)
         store(1, 1)
-        finish(early[1], "s")
-        finish_on_vector(multiply(0, 1, high, [2]))
-        store(1, 2)
-        finish(multiply(1, 1, low, [3]), "s")
-        finish_on_vector(multiply(3, 1, high, [3]))
-        store(1, 3)
+        finish(right_low[2], "s")
+        for place, experts, t in ((5, high, 2), (2, [6, 7], 3)):
+            if t == 3:
+                finish(multiply(4, 1, low, [3]), "s")
+                finish(multiply(3, 1, [4, 5], [3]), "s")
+            job = multiply(place, 1, experts, [t])
+            rectify_on_vector(job)
+            square_on_vector(job)
+            store(1, t)

@@ -313,27 +313,21 @@ def tile_moe_eps_lin_relu2_kernel(tc, xT, w_words, w_scales, b, offs, out):
             one_pass(job, 0)
         for job in right_low[:2]:
             one_pass(job, 1)
-        finish(right_low[0], "g")
-        finish(multiply(2, 1, [4, 5], [0]), "s")
-        waiting = [multiply(3, 1, [6], [0]), multiply(0, 1, [4, 5], [1]), multiply(7, 1, [7], [0])]
-        for job in waiting:
-            rectify_on_vector(job)
-        for job in (waiting[0], waiting[2]):
-            square_on_vector(job)
+        finish(right_low[0], "s")
+        first = [multiply(place, 1, experts, [0]) for place, experts in ((2, [4, 5]), (3, [6]), (7, [7]))]
+        for job in first:
+            add_bias(job)
+        for job in first:
+            square("v", 1, job[2], [0])
         store(1, 0)
-        finish(right_low[1], "g")
+        finish(right_low[1], "s")
+        right_high = multiply(0, 1, high, [1])
         one_pass(right_low[2], 1)
-        rest = multiply(1, 1, [6, 7], [1])
-        rectify_on_vector(rest)
-        for job in (waiting[1], rest):
-            square_on_vector(job)
+        finish_on_vector(right_high)
         store(1, 1)
         finish(right_low[2], "s")
-        for place, experts, t in ((5, high, 2), (2, [6, 7], 3)):
-            if t == 3:
-                finish(multiply(4, 1, low, [3]), "s")
-                finish(multiply(3, 1, [4, 5], [3]), "s")
-            job = multiply(place, 1, experts, [t])
-            rectify_on_vector(job)
-            square_on_vector(job)
-            store(1, t)
+        finish_on_vector(multiply(1, 1, high, [2]))
+        store(1, 2)
+        finish(multiply(5, 1, low, [3]), "s")
+        finish_on_vector(multiply(2, 1, high, [3]))
+        store(1, 3)

@@ -246,19 +246,21 @@ def tile_moe_eps_lin_relu2_kernel(tc, xT, w_words, w_scales, b, offs, out):
         quantize(0, 0, 256, 384)
         quantize(0, 0, 384, 512)
         load_bias(nc.gpsimd, keep.tile([P, N // P, E], F32, align_bytes=256, name="bias", tag="grouped00"))
-        word_tile(0, every, 0)
-        gather_words(0, every, [0])
+        word_tile(0, range(7), 0)
+        gather_words(0, range(7), [0])
         interleave(nc.scalar.copy, 0, 1, 0, 256)
         interleave(nc.scalar.copy, 0, 1, 256, 384, 256)
         interleave(nc.vector.tensor_copy, 0, 1, 384, 512, 256)
         quantize(0, 1, 0, 256)
         quantize(0, 1, 256, 512)
+        word_tile(0, [7], 0, "raw01_256")
+        gather_words(0, [7], [0])
         gather_scales(0, every)
-        word_tile(0, every, 1)
-        gather_words(0, every, [1])
+        word_tile(0, range(6), 1)
+        gather_words(0, range(6), [1])
         interleave(nc.scalar.copy, 1, 0, 0, 512)
         move_scales(0, nc.sync, every)
-        later = shared.tile([P, 24 * N], U8, align_bytes=256, name="later_weights", offset=0)
+        later = shared.tile([P, 24 * N], U8, align_bytes=256, name="later_weights", offset=2 * N)
         load_weight_words(later[:, : 4 * N], [2], range(4))
         load_weight_words(later[:, 4 * N : 8 * N], [3], range(4))
         load_weight_words(later[:, 8 * N : 12 * N], [4, 5], [0, 1])
@@ -267,9 +269,13 @@ def tile_moe_eps_lin_relu2_kernel(tc, xT, w_words, w_scales, b, offs, out):
         load_weight_words(later[:, 20 * N :], [6, 7], [2, 3])
         interleave(nc.scalar.copy, 1, 1, 0, 512)
         quantize(1, 0)
-        word_tile(1, range(3), 0)
-        gather_words(1, range(3), [0])
+        word_tile(0, [6, 7], 1, tile=shared.tile([P, 2 * P], U32, align_bytes=256, name="slot_words061", offset=0))
+        gather_words(0, [6, 7], [1])
+        word_tile(1, range(2), 0)
+        gather_words(1, range(2), [0])
         quantize(1, 1)
+        word_tile(1, [2], 0, "raw11_0")
+        gather_words(1, [2], [0])
         gather_scales(1, every)
         move_scales(1, nc.sync, every)
         word_tile(1, range(3, E), 0, "grouped11")
@@ -311,23 +317,21 @@ def tile_moe_eps_lin_relu2_kernel(tc, xT, w_words, w_scales, b, offs, out):
         right_low = [new_bank(place, 1, low, [t]) for t, place in enumerate((5, 4, 6))]
         for job in right_low:
             one_pass(job, 0)
-        for job in right_low[:2]:
-            one_pass(job, 1)
-        finish(right_low[0], "s")
-        first = [multiply(place, 1, experts, [0]) for place, experts in ((2, [4, 5]), (3, [6]), (7, [7]))]
-        for job in first:
-            add_bias(job)
-        for job in first:
-            square("v", 1, job[2], [0])
-        store(1, 0)
+        one_pass(right_low[0], 1)
+        finish(right_low[0], "g")
+        finish(multiply(2, 1, [4, 5], [0]), "s")
+        one_pass(right_low[1], 1)
         finish(right_low[1], "s")
-        right_high = multiply(0, 1, high, [1])
+        finish(multiply(3, 1, [4, 5], [1]), "s")
+        for place, e, tiles in ((7, 6, [0, 1]), (0, 7, [0]), (1, 7, [1])):
+            add_bias(multiply(place, 1, [e], tiles))
+        for t in (0, 1):
+            square("v", 1, [6, 7], [t])
+            store(1, t)
         one_pass(right_low[2], 1)
-        finish_on_vector(right_high)
-        store(1, 1)
         finish(right_low[2], "s")
-        finish_on_vector(multiply(1, 1, high, [2]))
+        finish_on_vector(multiply(5, 1, high, [2]))
         store(1, 2)
-        finish(multiply(5, 1, low, [3]), "s")
-        finish_on_vector(multiply(2, 1, high, [3]))
+        finish(multiply(2, 1, low, [3]), "s")
+        finish_on_vector(multiply(4, 1, high, [3]))
         store(1, 3)

@@ -42,6 +42,7 @@ def tile_moe_eps_lin_relu2_kernel(tc, xT, w_words, w_scales, b, offs, out):
         second = {}
         ww = {}
         ws = {}
+        apart = {}
 
         def load_x(h, a, lo=0, hi=HALF, tile=None):
             if tile is None:
@@ -78,9 +79,14 @@ def tile_moe_eps_lin_relu2_kernel(tc, xT, w_words, w_scales, b, offs, out):
             held["bias"] = tile
             queue.dma_start(held["bias"][:], b.rearrange("(t p) e -> p t e", p=P))
 
+        def rounded(h, a, lo, hi):
+            if (h, a, lo) in apart:
+                return apart[h, a, lo][:]
+            return grouped[h][a][:, lo:hi, :]
+
         def interleave(copy, h, a, lo, hi, base=0):
             copy(
-                out=grouped[h][a][:, lo:hi, :].rearrange("p (g i) j -> p g j i", i=4),
+                out=rounded(h, a, lo, hi).rearrange("p (g i) j -> p g j i", i=4),
                 in_=raw[h, a, base][:, :, lo - base : hi - base].rearrange("p j (g i) -> p g j i", i=4),
             )
 
@@ -89,7 +95,7 @@ def tile_moe_eps_lin_relu2_kernel(tc, xT, w_words, w_scales, b, offs, out):
             nc.vector.quantize_mx(
                 out=words[a][:, cols].bitcast(FP8X4),
                 scales=scales[4 * a : P, cols],
-                in_=grouped[h][a][:, lo:hi, :].rearrange("p w j -> p (w j)"),
+                in_=rounded(h, a, lo, hi).rearrange("p w j -> p (w j)"),
             )
 
         def gather(target, table, h, e):
@@ -232,8 +238,7 @@ def tile_moe_eps_lin_relu2_kernel(tc, xT, w_words, w_scales, b, offs, out):
         load_x(0, 1, 256, 512)
         load_x(1, 0, tile=shared.tile([P, 4, HALF], F32, align_bytes=256, name="raw10", offset=0))
         load_x(1, 1)
-        for e in (0, 1):
-            load_weight_words(byte_tile(f"first_weights{e}", 4 * N)[:], [e], range(4))
+        load_weight_words(byte_tile("first_weights", 4 * N)[:], [0], range(4))
 
         interleave(nc.vector.tensor_copy, 0, 0, 0, 128)
         interleave(nc.vector.tensor_copy, 0, 0, 128, 256)
@@ -260,42 +265,41 @@ def tile_moe_eps_lin_relu2_kernel(tc, xT, w_words, w_scales, b, offs, out):
         gather_words(0, range(6), [1])
         interleave(nc.scalar.copy, 1, 0, 0, 512)
         move_scales(0, nc.sync, every)
-        later = shared.tile([P, 24 * N], U8, align_bytes=256, name="later_weights", offset=2 * N)
-        load_weight_words(later[:, : 4 * N], [2], range(4))
-        load_weight_words(later[:, 4 * N : 8 * N], [3], range(4))
-        load_weight_words(later[:, 8 * N : 12 * N], [4, 5], [0, 1])
-        load_weight_words(later[:, 12 * N : 16 * N], [6, 7], [0, 1])
-        load_weight_words(later[:, 16 * N : 20 * N], [4, 5], [2, 3])
-        load_weight_words(later[:, 20 * N :], [6, 7], [2, 3])
-        interleave(nc.scalar.copy, 1, 1, 0, 512)
+        later = shared.tile([P, 28 * N], U8, align_bytes=256, name="later_weights", offset=2 * N)
+        loads = [([e], range(4)) for e in (1, 2, 3)] + [(pair, tiles) for tiles in ([0, 1], [2, 3]) for pair in ([4, 5], [6, 7])]
+        for i, (experts, tiles) in enumerate(loads):
+            load_weight_words(later[:, 4 * N * i : 4 * N * (i + 1)], experts, tiles)
+        interleave(nc.scalar.copy, 1, 1, 0, 256)
+        interleave(nc.scalar.copy, 1, 1, 256, 384)
         quantize(1, 0)
         word_tile(0, [6, 7], 1, tile=shared.tile([P, 2 * P], U32, align_bytes=256, name="slot_words061", offset=0))
         gather_words(0, [6, 7], [1])
-        word_tile(1, range(2), 0)
-        gather_words(1, range(2), [0])
-        quantize(1, 1)
-        word_tile(1, [2], 0, "raw11_0")
-        gather_words(1, [2], [0])
+        apart[1, 1, 384] = keep.tile([P, P, 4], BF16, align_bytes=256, name="last_share", tag="grouped10")
+        interleave(nc.vector.tensor_copy, 1, 1, 384, 512)
+        word_tile(1, [0], 0)
+        gather_words(1, [0], [0])
+        quantize(1, 1, 0, 256)
+        quantize(1, 1, 384, 512)
+        quantize(1, 1, 256, 384)
+        word_tile(1, [1], 0, "raw11_0")
+        gather_words(1, [1], [0])
         gather_scales(1, every)
         move_scales(1, nc.sync, every)
-        word_tile(1, range(3, E), 0, "grouped11")
+        word_tile(1, range(2, E), 0, "grouped11")
         word_tile(1, every, 1)
-        gather_words(1, [3], [0])
-        gather_words(1, low, [1])
-        gather_words(1, high, [1, 0])
+        gather_words(1, range(2), [1])
+        gather_words(1, range(2, E), [1, 0])
 
-        opening = [new_bank(e, 0, [e], range(4)) for e in (0, 1)]
+        opening = new_bank(0, 0, [0], range(4))
         for a in range(2):
-            for job in opening:
-                one_pass(job, a)
-        for job in opening:
-            rectify(job)
+            one_pass(opening, a)
+        rectify(opening)
+        rectify(multiply(1, 0, [1], range(4)))
         square("g", 0, [0, 1], [0, 1])
         for e in (2, 3):
             rectify(multiply(e, 0, [e], range(4)))
         square("g", 0, [2, 3], [0, 1])
-        for t in (2, 3):
-            square("g", 0, low, [t])
+        square("g", 0, low, [2])
         middle = multiply(4, 0, [4, 5], [0, 1])
         rectify(middle, 0)
         square("s", 0, [4, 5], [0])
@@ -307,30 +311,32 @@ def tile_moe_eps_lin_relu2_kernel(tc, xT, w_words, w_scales, b, offs, out):
         store(0, 1)
         middle = multiply(7, 0, [4, 5], [2, 3])
         rectify(middle, 2)
-        rectify(multiply(0, 0, [6, 7], [2]))
-        square("s", 0, high, [2])
+        square("g", 0, [4, 5], [2])
+        finish(multiply(0, 0, [6, 7], [2]), "s")
         store(0, 2)
+        square("g", 0, low, [3])
         rectify(middle, 3)
-        square("g", 0, [4, 5], [3])
-        finish(multiply(1, 0, [6, 7], [3]), "s")
+        rectify(multiply(1, 0, [6, 7], [3]))
+        square("s", 0, high, [3])
         store(0, 3)
-        right_low = [new_bank(place, 1, low, [t]) for t, place in enumerate((5, 4, 6))]
-        for job in right_low:
-            one_pass(job, 0)
-        one_pass(right_low[0], 1)
-        finish(right_low[0], "g")
-        finish(multiply(2, 1, [4, 5], [0]), "s")
-        one_pass(right_low[1], 1)
-        finish(right_low[1], "s")
-        finish(multiply(3, 1, [4, 5], [1]), "s")
-        for place, e, tiles in ((7, 6, [0, 1]), (0, 7, [0]), (1, 7, [1])):
-            add_bias(multiply(place, 1, [e], tiles))
-        for t in (0, 1):
-            square("v", 1, [6, 7], [t])
-            store(1, t)
-        one_pass(right_low[2], 1)
-        finish(right_low[2], "s")
-        finish_on_vector(multiply(5, 1, high, [2]))
+        finish(multiply(2, 1, low, [0]), "s")
+        early = multiply(3, 1, low, [1])
+        first = [multiply(4, 1, [4, 5], [0])]
+        second_tile = fill(new_bank(5, 1, high, [1]), [4, 5])
+        for place, e in ((6, 6), (0, 7)):
+            first.append(multiply(place, 1, [e], [0]))
+            fill(second_tile, [e])
+        for job in first:
+            add_bias(job)
+        for job in first:
+            square("v", 1, job[2], [0])
+        store(1, 0)
+        finish(early, "s")
+        later_low = multiply(7, 1, low, [2])
+        finish_on_vector(second_tile)
+        store(1, 1)
+        finish(later_low, "s")
+        finish_on_vector(multiply(1, 1, high, [2]))
         store(1, 2)
         finish(multiply(2, 1, low, [3]), "s")
         finish_on_vector(multiply(4, 1, high, [3]))

from contextlib import ExitStack

import concourse.mybir as mybir

K, T, E, C, N, R = 1024, 1024, 8, 256, 512, 8
U = C // R
P = 128
HALF = T // 2
FLOPS = 2 * E * C * K * N

F32 = mybir.dt.float32
BF16 = mybir.dt.bfloat16
I32 = mybir.dt.int32
U32 = mybir.dt.uint32
U16 = mybir.dt.uint16
U8 = mybir.dt.uint8
FP8X4 = mybir.dt.float8_e4m3fn_x4
FP4X4 = mybir.dt.float4_e2m1fn_x4
RELU = mybir.ActivationFunctionType.Relu
SQUARE = mybir.ActivationFunctionType.Square
MULT = mybir.AluOpType.mult
ADD = mybir.AluOpType.add
MAX = mybir.AluOpType.max


def tile_moe_eps_lin_relu2_kernel(tc, xT, w_words, w_scales, b, offs, out):
    nc = tc.nc
    with ExitStack() as ctx:
        keep = ctx.enter_context(tc.tile_pool(name="keep", bufs=1))
        shared = ctx.enter_context(tc.tile_pool(name="shared", bufs=1))
        psum = ctx.enter_context(tc.psum_pool(name="psum", bufs=1))

        offsets = keep.tile([P, E * C // 16], U16, name="offsets")
        raw = {}
        grouped = [[keep.tile([P, HALF, 4], BF16, align_bytes=256, name=f"grouped{h}{a}") for a in range(2)] for h in range(2)]
        words = [keep.tile([P, T], U32, align_bytes=256, name=f"words{a}") for a in range(2)]
        scales = keep.tile([P, T], U8, align_bytes=256, name="scales")
        both = {}
        held = {}
        results = [keep.tile([P, 4, R // 2, E, U], F32, name=f"results{h}") for h in range(2)]
        slot_words = {}
        second = {}
        ww = {}
        ws = {}
        apart = {}

        def load_x(h, a, lo=0, hi=HALF, tile=None):
            if tile is None:
                tile = keep.tile([P, 4, hi - lo], F32, align_bytes=256, name=f"raw{h}{a}_{lo}", tag=f"raw{h}{a}_{lo}")
            raw[h, a, lo] = tile
            rows = xT[512 * a : 512 * (a + 1), HALF * h + lo : HALF * h + hi]
            nc.sync.dma_start(raw[h, a, lo][:], rows.rearrange("(p j) w -> p j w", j=4))

        def load_weight_scales(queue, tile, experts):
            lo, n = experts[0], len(experts)
            rows = w_scales[lo : lo + n].bitcast(I32).rearrange("e a (q r) n -> r q (e a) n", r=4)
            for r in range(4):
                queue.dma_start(tile[r:P:32, :].bitcast(I32).rearrange("q (x n) -> q x n", x=2 * n), rows[r])
            for e in experts:
                ws[e] = tile[:, (e - lo) * 2 * N : (e - lo + 1) * 2 * N]

        def load_weight_words(tile, experts, tiles):
            lo, n, width = experts[0], len(experts), 2 * P * len(tiles)
            rows = w_words[lo : lo + n, :, :, 2 * P * tiles[0] : 2 * P * (tiles[-1] + 1)]
            nc.sync.dma_start(
                tile.bitcast(I32).rearrange("p (x n) -> p x n", x=2 * n),
                rows.bitcast(I32).rearrange("e a p n -> p (e a) n"),
            )
            for e in experts:
                for a in range(2):
                    for t in tiles:
                        first = (2 * (e - lo) + a) * width + 2 * P * (t - tiles[0])
                        ww[e, a, t] = tile[:, first : first + 2 * P]

        def byte_tile(name, width, tag=None):
            return keep.tile([P, width], U8, align_bytes=256, name=name, tag=tag or name)

        def load_bias(queue, tile):
            held["bias"] = tile
            queue.dma_start(held["bias"][:], b.rearrange("(t p) e -> p t e", p=P))

        def rounded(h, a, lo, hi):
            if (h, a, lo) in apart:
                return apart[h, a, lo][:]
            return grouped[h][a][:, lo:hi, :]

        def interleave(copy, h, a, lo, hi, base=0):
            copy(
                out=rounded(h, a, lo, hi).rearrange("p (g i) j -> p g j i", i=4),
                in_=raw[h, a, base][:, :, lo - base : hi - base].rearrange("p j (g i) -> p g j i", i=4),
            )

        def quantize(h, a, lo=0, hi=HALF):
            cols = slice(HALF * h + lo, HALF * h + hi)
            nc.vector.quantize_mx(
                out=words[a][:, cols].bitcast(FP8X4),
                scales=scales[4 * a : P, cols],
                in_=rounded(h, a, lo, hi).rearrange("p w j -> p (w j)"),
            )

        def gather(target, table, h, e):
            first = (C * e + P * h) // 16
            window = table[:, : HALF * (h + 1)]
            nc.vector.tensor_copy(target, window.indirect(offsets[:, first : first + P // 16]))

        def word_tile(h, experts, a, tag=None, tile=None):
            name = f"slot_words{h}{experts[0]}{a}"
            if tile is None:
                tile = keep.tile([P, len(experts) * P], U32, align_bytes=256, name=name, tag=tag or name)
            for i, e in enumerate(experts):
                slot_words[h, e, a] = tile[:, P * i : P * (i + 1)]

        def gather_words(h, experts, passes):
            for e in experts:
                for a in passes:
                    gather(slot_words[h, e, a], words[a], h, e)

        def gather_scales(h, experts, tile=None):
            if tile is None:
                tile = byte_tile(f"both{h}{experts[0]}", len(experts) * P)
            for i, e in enumerate(experts):
                both[h, e] = tile[:, P * i : P * (i + 1)]
                gather(both[h, e], scales, h, e)
            both[h, experts[0], "all"] = tile

        def move_scales(h, queue, experts, tile=None):
            lo, n = experts[0], len(experts)
            if tile is None:
                tile = keep.tile([P, n * P], U8, align_bytes=256, name=f"second{h}{lo}")
            for r in range(4):
                queue.dma_start(tile[r:P:32, :].bitcast(I32), both[h, lo, "all"][r + 4 : P : 32, :].bitcast(I32))
            for e in experts:
                second[h, e] = tile[:, P * (e - lo) : P * (e - lo + 1)]

        def product(target, h, e, t, a, start, stop):
            nc.tensor.matmul_mx(
                out=target,
                lhsT=ww[e, a, t].bitcast(FP4X4),
                lhsT_scale=ws[e][:, N * a + P * t : N * a + P * (t + 1)],
                rhs=slot_words[h, e, a].bitcast(FP8X4),
                rhs_scale=second[h, e] if a == 1 else both[h, e],
                start=start,
                stop=stop,
            )

        def new_bank(place, h, experts, tiles):
            bank = psum.tile([P, len(experts), len(tiles), P], F32, name="bank", tag=f"bank{place}")
            return bank, h, experts, tiles

        def fill(job, some):
            bank, h, experts, tiles = job
            for e in some:
                for j, t in enumerate(tiles):
                    product(bank[:, experts.index(e), j, :], h, e, t, 1, True, False)
                    product(bank[:, experts.index(e), j, :], h, e, t, 0, False, True)
            return job

        def multiply(place, h, experts, tiles):
            return fill(new_bank(place, h, experts, tiles), experts)

        def one_pass(job, a):
            bank, h, experts, tiles = job
            sums = [(i, e, j, t) for i, e in enumerate(experts) for j, t in enumerate(tiles)]
            for n, (i, e, j, t) in enumerate(sums):
                product(bank[:, i, j, :], h, e, t, a, a == 0 and n == 0, a == 1 and n == len(sums) - 1)

        def rectify(job, only=None, stage=None):
            bank, h, experts, tiles = job
            for j, t in enumerate(tiles):
                for i, e in enumerate(experts if only in (None, t) else []):
                    sums = bank[:, i, j, :].rearrange("p (m u) -> p m u", u=U)
                    target = results[h][:, t, :, e, :] if stage is None else stage[:, :, i, :]
                    nc.scalar.activation(target, sums, RELU, bias=held["bias"][:, t, e : e + 1])

        def add_bias(job):
            bank, h, experts, tiles = job
            if len(tiles) == 1:
                t, es = tiles[0], slice(experts[0], experts[-1] + 1)
                target = results[h][:, t, :, es, :].rearrange("p m e u -> p e m u")
                sums = bank[:, :, 0, :].rearrange("p e (m u) -> p e m u", u=U)
                spread = held["bias"][:, t, es].unsqueeze(2).unsqueeze(3).to_broadcast([P, len(experts), R // 2, U])
                nc.vector.tensor_tensor(target, sums, spread, ADD)
            else:
                ts = slice(tiles[0], tiles[-1] + 1)
                for i, e in enumerate(experts):
                    sums = bank[:, i, :, :].rearrange("p t (m u) -> p t m u", u=U)
                    spread = held["bias"][:, ts, e].unsqueeze(2).unsqueeze(3).to_broadcast([P, len(tiles), R // 2, U])
                    nc.vector.tensor_tensor(results[h][:, ts, :, e, :], sums, spread, ADD)

        def square(engine, h, experts, tiles):
            v = results[h][:, tiles[0] : tiles[-1] + 1, :, experts[0] : experts[-1] + 1, :].rearrange("p t m e u -> p (t m) (e u)")
            if engine == "s":
                nc.scalar.activation(v, v, SQUARE)
            elif engine == "v":
                nc.vector.scalar_tensor_tensor(v, v, 0.0, v, MAX, MULT)
            else:
                nc.gpsimd.tensor_tensor(v, v, v, MULT)

        def finish(job, engine):
            rectify(job)
            square(engine, job[1], job[2], job[3])

        def finish_on_vector(job):
            bank, h, experts, tiles = job
            pairs = [(bank[:, i : min(i + 2, len(experts))], h, experts[i : i + 2], tiles) for i in range(0, len(experts), 2)]
            for pair in pairs:
                add_bias(pair)
            for pair in pairs:
                square("v", h, pair[2], tiles)

        def parts(job):
            bank, h, experts, tiles = job
            return [
                (results[h][:, t, :, e, :], bank[:, i, j, :].rearrange("p (m u) -> p m u", u=U), held["bias"][:, t, e : e + 1])
                for i, e in enumerate(experts)
                for j, t in enumerate(tiles)
            ]

        def rectify_on_vector(job):
            for target, sums, column in parts(job):
                nc.vector.tensor_scalar(target, sums, column, 0.0, ADD, MAX)

        def square_on_vector(job):
            for target, sums, column in parts(job):
                nc.vector.scalar_tensor_tensor(target, sums, column, target, ADD, MULT)

        def store(h, t):
            rows = out[P * t : P * (t + 1), T * h : T * (h + 1)]
            nc.sync.dma_start(rows, results[h][:, t].rearrange("p m e u -> p (m e u)"))

        every, low, high = range(E), range(4), range(4, E)
        nc.gpsimd.memset(scales[:].bitcast(I32), 0)

        load_x(0, 0, 0, 384)
        load_x(0, 0, 384, 512)
        nc.sync.dma_start(offsets[:], offs)
        load_x(0, 1, 0, 256)
        load_x(0, 1, 256, 512)
        load_x(1, 0, tile=shared.tile([P, 4, HALF], F32, align_bytes=256, name="raw10", offset=0))
        load_x(1, 1)
        load_weight_words(byte_tile("first_weights", 4 * N)[:], [0], range(4))

        interleave(nc.vector.tensor_copy, 0, 0, 0, 128)
        interleave(nc.vector.tensor_copy, 0, 0, 128, 256)
        interleave(nc.scalar.copy, 0, 0, 256, 384)
        quantize(0, 0, 0, 128)
        quantize(0, 0, 128, 256)
        interleave(nc.vector.tensor_copy, 0, 0, 384, 464, 384)
        interleave(nc.scalar.copy, 0, 0, 464, 512, 384)
        load_weight_scales(nc.gpsimd, byte_tile("weight_scales", 16 * N, "raw00_384")[:], every)
        quantize(0, 0, 256, 384)
        quantize(0, 0, 384, 512)
        load_bias(nc.gpsimd, keep.tile([P, N // P, E], F32, align_bytes=256, name="bias", tag="grouped00"))
        word_tile(0, range(7), 0)
        gather_words(0, range(7), [0])
        interleave(nc.scalar.copy, 0, 1, 0, 256)
        interleave(nc.scalar.copy, 0, 1, 256, 384, 256)
        interleave(nc.vector.tensor_copy, 0, 1, 384, 512, 256)
        quantize(0, 1, 0, 256)
        quantize(0, 1, 256, 512)
        word_tile(0, [7], 0, "raw01_256")
        gather_words(0, [7], [0])
        gather_scales(0, every)
        word_tile(0, range(6), 1)
        gather_words(0, range(6), [1])
        interleave(nc.scalar.copy, 1, 0, 0, 512)
        move_scales(0, nc.sync, every)
        later = shared.tile([P, 28 * N], U8, align_bytes=256, name="later_weights", offset=2 * N)
        loads = [([e], range(4)) for e in (1, 2, 3)] + [(pair, tiles) for tiles in ([0, 1], [2, 3]) for pair in ([4, 5], [6, 7])]
        for i, (experts, tiles) in enumerate(loads):
            load_weight_words(later[:, 4 * N * i : 4 * N * (i + 1)], experts, tiles)
        interleave(nc.scalar.copy, 1, 1, 0, 256)
        interleave(nc.scalar.copy, 1, 1, 256, 384)
        quantize(1, 0)
        word_tile(0, [6, 7], 1, tile=shared.tile([P, 2 * P], U32, align_bytes=256, name="slot_words061", offset=0))
        gather_words(0, [6, 7], [1])
        apart[1, 1, 384] = keep.tile([P, P, 4], BF16, align_bytes=256, name="last_share", tag="grouped10")
        interleave(nc.vector.tensor_copy, 1, 1, 384, 512)
        word_tile(1, [0], 0)
        gather_words(1, [0], [0])
        quantize(1, 1, 0, 256)
        quantize(1, 1, 384, 512)
        quantize(1, 1, 256, 384)
        word_tile(1, [1], 0, "raw11_0")
        gather_words(1, [1], [0])
        gather_scales(1, every)
        move_scales(1, nc.sync, every)
        word_tile(1, range(2, E), 0, "grouped11")
        word_tile(1, every, 1)
        gather_words(1, range(2), [1])
        gather_words(1, range(2, E), [1, 0])

        opening = new_bank(0, 0, [0], range(4))
        for a in range(2):
            one_pass(opening, a)
        rectify(opening)
        rectify(multiply(1, 0, [1], range(4)))
        square("g", 0, [0, 1], [0, 1])
        for e in (2, 3):
            rectify(multiply(e, 0, [e], range(4)))
        square("g", 0, [2, 3], [0, 1])
        square("g", 0, low, [2])
        middle = multiply(4, 0, [4, 5], [0, 1])
        rectify(middle, 0)
        square("s", 0, [4, 5], [0])
        finish(multiply(5, 0, [6, 7], [0]), "s")
        store(0, 0)
        rectify(middle, 1)
        rectify(multiply(6, 0, [6, 7], [1]))
        square("s", 0, high, [1])
        store(0, 1)
        middle = multiply(7, 0, [4, 5], [2, 3])
        rectify(middle, 2)
        square("g", 0, [4, 5], [2])
        finish(multiply(0, 0, [6, 7], [2]), "s")
        store(0, 2)
        square("g", 0, low, [3])
        rectify(middle, 3)
        rectify(multiply(1, 0, [6, 7], [3]))
        square("s", 0, high, [3])
        store(0, 3)
        finish(multiply(2, 1, low, [0]), "s")
        early = multiply(3, 1, low, [1])
        first = [multiply(4, 1, [4, 5], [0])]
        second_tile = fill(new_bank(5, 1, high, [1]), [4, 5])
        for place, e in ((6, 6), (0, 7)):
            first.append(multiply(place, 1, [e], [0]))
            fill(second_tile, [e])
        for job in first:
            add_bias(job)
        for job in first:
            square("v", 1, job[2], [0])
        store(1, 0)
        finish(early, "s")
        later_low = multiply(7, 1, low, [2])
        finish_on_vector(second_tile)
        store(1, 1)
        finish(later_low, "s")
        finish_on_vector(multiply(1, 1, high, [2]))
        store(1, 2)
        finish(multiply(2, 1, low, [3]), "s")
        finish_on_vector(multiply(4, 1, high, [3]))
        store(1, 3)
